import numpy as np, ml_dtypes
CORES = [1,5,17,21,33,37,49,53]
N = 8
import mx_ref
BF = ml_dtypes.bfloat16
def gcols(t, e):
    v = np.concatenate([t.reshape(8, 16, -1, 4), np.zeros((8, 16, 1, 4), BF)], axis=2)
    return np.ascontiguousarray(np.stack([v[g][:, e[g]] for g in range(8)])).reshape(128, -1)
def tile(rs):
    return np.stack(rs, axis=2).reshape(128, -1).astype(BF)
def cut(t, i, w=512):
    return t[:, w * i:w * i + w]
def pick(q, e):
    c = np.concatenate([q[0].reshape(128, -1, 4), np.zeros((128, 1, 4), np.uint8)], axis=1); s = np.concatenate([q[1], np.ones((16, 1), np.uint8)], axis=1)
    return (np.ascontiguousarray(c[:, e].reshape(128, -1)), np.ascontiguousarray(s[:, e]))
def join(*qs):
    return (np.concatenate([q[0] for q in qs], axis=1), np.concatenate([q[1] for q in qs], axis=1))
def put(q, e, v):
    c, s = q[0].reshape(128, -1, 4).copy(), q[1].copy(); c[:, e] = v[0].reshape(128, -1, 4); s[:, e] = v[1]
    return (c.reshape(128, -1), s)
def pk(c, s):
    return (np.ascontiguousarray(c), mx_ref.live(s))
def emit(q):
    return q[0], q[1]
def packed(v, rng):
    q = [mx_ref.quantize(np.ascontiguousarray(v[r])) for r in range(N)]
    return np.stack([a for a, b in q]), np.stack([mx_ref.plane(b, rng) for a, b in q])
def values_of_codes():
    e, c = np.zeros((128, 128, 4), np.float32), np.zeros((128, 2, 4), np.uint8)
    e[np.arange(128), np.arange(128), 0] = 1
    c[:127, :, 0] = np.arange(256).reshape(2, 128).T[:127]
    return mx_ref.matmul(mx_ref.quantize(e.reshape(128, 512).astype(BF)), (c.reshape(128, 8), np.full((16, 2), 127, np.uint8))).T.reshape(-1).astype(np.float64)
CODE_VALUE, SCALE_VALUE = values_of_codes(), 2.0 ** (np.arange(256) - 127.0)
def decode(q):
    return (CODE_VALUE[q[0]].reshape(16, 8, -1, 4) * SCALE_VALUE[q[1]][:, None, :, None] + 0.0).reshape(128, -1).astype(np.float32)
def f(rng, *shape):
    return mx_ref.flush((rng.standard_normal(shape, dtype=np.float32) * np.exp2(rng.integers(-2, 3, shape[:-1] + (1,)))).astype(BF))
def wide(rng, *shape, cols=0):
    v = rng.standard_normal(shape, dtype=np.float32) * np.exp2(rng.integers(-12, 13, shape)).astype(np.float32)
    if cols: v *= np.repeat(np.exp2(rng.integers(-cols, cols + 1, shape[:-2] + (1, shape[-1] // 4))) * (rng.random(shape[:-2] + (1, shape[-1] // 4)) > 0.0625), 4, axis=-1).astype(np.float32)
    return mx_ref.flush(v.astype(BF))
C, H, R, STEP = 320, 128, 3, 11
def big(v):
    v = v.astype(np.float32)
    v[np.abs(v) < np.float32(2.0 ** -16)] = 0
    return v.astype(BF)
def numbers_of(rng):
    return {"x": big(f(rng, N, 128, 4 * C)), "u": np.array(f(rng, N, 128, 512)), "v": np.array(f(rng, N, 128, 512))}
def plays(rng):
    return rng.integers(1, 7, (N, 8, 1)).astype(np.int32)
def layers(rng):
    return big(f(rng, N, 128, 2048)).reshape(N, 8, 16, 4, 8, 16, 4)
def weights(rng, w):
    c, s = packed(np.ascontiguousarray(w).reshape(N, 128, 2048), rng)
    return {"wc": c, "ws": s}
def turning(rng):
    b = np.abs(128 - (STEP * np.arange(130)) % 256)
    k = np.flatnonzero((b[1:129] - b[:128]) * (b[2:] - b[1:129]) < 0) + 1
    e = min(STEP, C // 32) - 1
    k = np.concatenate([[0], k[:e], [128]])
    s = -np.ones(C)
    for i in range(e + 1):
        lo = 32 * i
        hi = lo + 32 if i < e else C
        m = [lo, hi - 1]
        w = rng.permutation(np.setdiff1d(np.arange(lo, hi), m))
        s[m] = 1
        s[w[:k[i + 1] - k[i] - len(m)]] = 1
    return s
def setup_inputs(rng):
    return {**numbers_of(rng), "p": plays(rng), **weights(rng, layers(rng))}
def setup_inputs_ties(rng):
    d = numbers_of(rng)
    e = rng.permutation(N)
    x = d["x"].reshape(N, 8, 16, C, 4)
    a = (1.0 + (2 * rng.integers(0, 64, (N, 8, 8, C, 4)) + 1) * 2.0 ** -7) * np.exp2(-rng.integers(8, 15, (N, 8, 8, C, 4)).astype(np.float64))
    a *= rng.integers(0, 2, a.shape) * 2.0 - 1.0
    a[:, :, 0, :, 0] = 1.96875
    x[:, :, 8:] = a.astype(np.float32).astype(BF)
    for r in range(N):
        k = rng.permutation(C) % 3
        if r == e[0]: k = np.ones(C, int)
        elif r in e[2::2]: k = rng.permutation(3)[np.arange(C) % 3]
        c = x[r, 0, :8, :3].copy()
        c[:, 0] = 0
        c[:, 2] = -c[:, 1]
        x[r, 0, :8] = c[:, k]
    x[e[1]] = 0
    u = d["u"].reshape(N, 8, 16, 128, 4)
    u[:, 1:, :, 0] = 0
    u[:, 0, 8:, 0] = 0
    w = layers(rng)
    w[:, :, :, :, 0, :8] = 0
    return {"x": x.reshape(N, 128, 4 * C), "u": u.reshape(N, 128, 512), "v": d["v"], "p": plays(rng), **weights(rng, w)}
def setup_inputs_near(rng):
    d = numbers_of(rng)
    x = d["x"].reshape(N, 8, 16, C, 4)
    u = d["u"].reshape(N, 128, 128, 4)
    o = rng.permutation(N) % 2
    x[:, 0, 0] = 0
    x[:, 0, 8:] = 0
    u[:, :, 0] = 0
    for r in range(N):
        k = 2.0 ** -30 if o[r] == 0 else 1.0
        c = rng.permutation(C) % 3
        x[r, 0, 8, :, 0] = (np.array([9, 8, 9])[c] * 0.125 * k).astype(np.float32).astype(BF)
        x[r, 0, 9, :, 0] = (np.array([10, 9, 11])[c] * 0.125 * k).astype(np.float32).astype(BF)
        x[r, 0, 0, rng.integers(C), 0] = 2.0 ** 29 * (rng.integers(0, 2) * 2.0 - 1.0)
        u[r, 0, 0, 0] = k
        u[r, 8, 0, 0] = 1.125 * k
        u[r, 9, 0, 0] = -k
    w = layers(rng)
    for i in [0] + [8 + j for j in range(8)]:
        w[:, 0, i] = 0
        w[:, :, :, :, 0, i] = 0
    return {"x": x.reshape(N, 128, 4 * C), "u": u.reshape(N, 128, 512), "v": d["v"], "p": plays(rng), **weights(rng, w)}
def setup_inputs_late(rng):
    d = numbers_of(rng)
    x = d["x"].reshape(N, 128, C, 4)
    k = rng.permutation(N) % 2
    c = (k * 2.0 - 1.0).astype(np.float32).astype(BF)
    x[:, 0] = c[:, None, None]
    x[:, 1:8] = np.clip(x[:, 1:8].astype(np.float32), -8, 8).astype(BF)
    u = d["u"].reshape(N, 128, 128, 4)
    u[:, :, 0] = 0
    u[:, 0, 0, 0] = 1
    p = plays(rng)
    p[k == 0, 0] = 1
    p[np.flatnonzero(k == 1)[0]] = 6
    return {"x": x.reshape(N, 128, 4 * C), "u": u.reshape(N, 128, 512), "v": d["v"], "p": p, **weights(rng, layers(rng))}
def setup_inputs_ends(rng):
    d = numbers_of(rng)
    x = np.zeros((N, 8, 16, C, 4), np.float32)
    u = d["u"].reshape(N, 128, 128, 4)
    v = d["v"]
    o = rng.permutation(N) % 4
    for t in range(N):
        for r in range(N):
            if o[r] == 3 and o[(r + 1) % N] == 2:
                o[r] = 2
                o[(r + 1) % N] = 3
    h = rng.permutation(N) % 2
    m = np.flatnonzero(o == 1)
    if (h[m] == 0).all():
        h[np.flatnonzero(h == 1)[0]] = 0
        h[m[0]] = 1
    p = np.zeros((N, 8, 1), np.int32)
    w = np.zeros((N, 128, 4, 128, 4), np.float32)
    i = np.arange(128)
    u[:, :, 0] = 0
    for r in range(N):
        p[r] = 6 if h[r] == 0 else 1
        for b in range(4): w[r, i, b, i, b] = 1 if o[r] == 3 else -1
        if o[r] < 3:
            a = rng.integers(8, 17, (8, 1, C, 1)) * 2.0 ** 26
            x[r] = a if o[r] == 0 else -a if o[r] == 1 else a * turning(rng)[None, None, :, None]
            u[r, :, 0] = 2.0 ** 30
        else:
            x[r] = rng.integers(8, 16, (8, 1, C, 1)) * 2.0 ** -33
            x[r, 0, 0, :, 0] = (2 + rng.permutation(C) % 3) * 2.0 ** -31
            x[r, 0, 1, :, 0] = 2.0 ** -30
            u[r, 0, 0, 0] = 2.0 ** -30
            u[r, 1, 0, 0] = -1.5 * 2.0 ** -30
        if o[r] in (0, 2): v[r] = (2.0 ** 30 * (rng.integers(0, 2, (128, 512)) * 2.0 - 1.0)).astype(np.float32).astype(BF)
        if o[r] == 3: v[r] = 2.0 ** -30
    return {"x": x.reshape(N, 128, 4 * C).astype(BF), "u": u.reshape(N, 128, 512), "v": v, "p": p, **weights(rng, w.astype(BF))}
def setup_inputs_spread(rng):
    d = setup_inputs(rng)
    d["x"] = big(wide(rng, N, 128, 4 * C, cols=6))
    return d
def check_inputs(d):
    b = []
    for k in ("x", "u", "v"):
        a = np.abs(d[k].astype(np.float32))
        if not (np.isfinite(a).all() and ((a == 0) | (a >= 2.0 ** -30) & (a <= 2.0 ** 30)).all()): b.append("a value of " + k)
    if not ((d["p"] >= 1) & (d["p"] <= 6)).all(): b.append("an entry of p")
    none, least, most = [emit(mx_ref.quantize(np.full((128, 16), k, np.float32).astype(BF)))[1][0, 0] for k in (0.0, 2.0 ** -30, 2.0 ** 30)]
    for r in range(N):
        if ((d["wc"][r] == 0x7F) | (d["wc"][r] == 0xFF)).any(): b.append("wc: a code that is no number")
        s = mx_ref.live(d["ws"][r])
        if ((s != none) & ((s < least) | (s > most))).any(): b.append("ws: a scale out of range")
    return b
def reference(x, u, v, p, wc, ws):
    qu = [mx_ref.quantize(u[r]) for r in range(N)]
    lay = [pk(wc[r], ws[r]) for r in range(N)]
    now = [x[r] for r in range(N)]
    n, kept = np.zeros(N, np.int64), np.zeros((N, 8), np.int64)
    a = np.zeros((N, 8, C), np.int64)
    for t in range(R):
        q = [mx_ref.quantize(now[r]) for r in range(N)]
        held = [decode(q[r]).astype(BF) for r in range(N)]
        s = np.stack([mx_ref.matmul(qu[r], q[r])[0] > 0 for r in range(N)])
        for j in range(C):
            n = n + s[:, j]
            c = np.abs(128 - (STEP * n) % 256)
            for g in range(8):
                c = np.minimum(np.maximum(kept[:, g], c - p[:, g, 0]), c + p[:, g, 0])
                kept[:, g] = c
            a[:, :, j] = kept
        made = []
        for r in range(N):
            window = np.concatenate([held[r], cut(held[(r + 1) % N], 0, 4 * H)], axis=1)
            far = gcols(window, np.arange(C) + a[r])
            z = mx_ref.quantize(((held[r].astype(np.float32) + far.astype(np.float32)) * np.float32(0.5)).astype(BF))
            made.append(tile([mx_ref.matmul(pick(lay[r], np.arange(128 * b, 128 * b + 128)), z) * np.float32(0.03125) + now[r][:, b::4].astype(np.float32) for b in range(4)]))
        now = made
    y, ao = np.zeros((N, 128, C), np.float32), np.zeros((N, 8, C), np.float32)
    oc, osc = np.zeros((N, 128, 4 * C), np.uint8), np.zeros((N, 16, C), np.uint8)
    for r in range(N):
        q = mx_ref.quantize(now[r])
        y[r] = mx_ref.matmul(mx_ref.quantize(v[r]), q)
        ao[r] = a[r]
        oc[r], osc[r] = emit(q)
    return {"y": y, "ao": ao, "oc": oc, "osc": osc}

@@ -1,0 +1,407 @@
+from concourse.mybir import dt, AluOpType, ActivationFunctionType, AxisListType
+
+N = 8
+CA, CB, C, H, W = 192, 128, 320, 128, 448
+LO = {"A": 0, "B": CA}
+NC = {"A": CA, "B": CB}
+ROUNDS = 3
+TINY = 2.0 ** -30
+BASE = 49152.0
+
+F32, B16, I32, U16, U8, X4 = "float32", "bfloat16", "int32", "uint16", "uint8", "float8_e4m3fn_x4"
+SCRATCH = {
+    "ut": ("sbuf", [128, 512], B16), "vt": ("sbuf", [128, 512], B16),
+    "cu": ("sbuf", [128, 128], X4), "su": ("sbuf", [128, 128], U8),
+    "cu0": ("sbuf", [128, 128], X4), "su0": ("sbuf", [128, 128], U8),
+    "cv": ("sbuf", [128, 128], X4), "sv": ("sbuf", [128, 128], U8),
+    "cw": ("sbuf", [128, 512], X4), "sw": ("sbuf", [128, 512], U8),
+    "eb": ("sbuf", [128, 516], B16), "ce": ("sbuf", [128, 512], X4), "se": ("sbuf", [128, 512], U8),
+    "offz": ("sbuf", [128, 8], U16), "zero": ("sbuf", [128, CA], B16),
+    "mi": ("sbuf", [128, CA], I32), "mask": ("sbuf", [128, CA], B16), "hit": ("sbuf", [128, 16], B16),
+    "rs": ("sbuf", [128, 16], F32), "sc": ("sbuf", [128, 1], F32),
+    "pid": ("sbuf", [128, 12], I32), "kk": ("sbuf", [128, 12], F32), "kt": ("sbuf", [128, 12], F32),
+    "prow": ("sbuf", [1, 8], I32), "pf": ("sbuf", [1, 8], F32), "pb": ("sbuf", [128, 8], F32),
+    "ps": ("sbuf", [128, 1], F32), "pp": ("sbuf", [128, 1], B16),
+    "xi": ("sbuf", [128, 1], F32),
+    "fl": ("sbuf", [128, C], B16), "yA": ("sbuf", [128, CA + 8], B16), "yB": ("sbuf", [128, CB + 8], B16),
+    "dy": ("sbuf", [128, C], B16), "ee": ("sbuf", [128, C], B16), "ae": ("sbuf", [128, C], B16),
+    "d0": ("sbuf", [128, C], B16), "d1": ("sbuf", [128, C], B16), "pl": ("sbuf", [128, C], B16),
+    "sm": ("sbuf", [128, C], B16), "o1": ("sbuf", [128, 20], F32),
+    "aof": ("sbuf", [128, C], F32), "yo": ("sbuf", [128, C], F32),
+}
+for _t in range(ROUNDS + 1):
+    SCRATCH["xt%d" % _t] = ("sbuf", [128, 4 * C], B16)
+    SCRATCH["cx%d" % _t] = ("sbuf", [128, C], X4)
+    SCRATCH["sx%d" % _t] = ("sbuf", [128, C], U8)
+for _t in range(ROUNDS):
+    SCRATCH["lc%d" % _t] = ("sbuf", [128, H], X4)
+    SCRATCH["ls%d" % _t] = ("sbuf", [128, H], U8)
+    SCRATCH["zt%d" % _t] = ("sbuf", [128, 4 * C], B16)
+    SCRATCH["cz%d" % _t] = ("sbuf", [128, C], X4)
+    SCRATCH["sz%d" % _t] = ("sbuf", [128, C], U8)
+    SCRATCH["off%d" % _t] = ("sbuf", [128, 20], U16)
+for _t in range(2):
+    for _b in range(4):
+        SCRATCH["w%d%d" % (_t, _b)] = ("sbuf", [128, W], B16)
+        SCRATCH["fn"[_b < 2] + "%d%d" % (_t, _b)] = ("sbuf", [128, C], B16)
+for _b in range(8):
+    SCRATCH["bank%d" % _b] = ("psum", [128, 512], F32)
+NDMA = 18
+SEMAPHORES = ["c_pe", "c_v", "c_s", "c_g"] + ["dma%d" % _i for _i in range(NDMA)] + ["arr%d" % _t for _t in range(ROUNDS)] + ["left%d" % _t for _t in range(ROUNDS)]
+
+
+def rank_program(g, core, T, topo):
+    rank = T.rank_of(core)
+    if rank is None:
+        return
+    A, ACT = AluOpType, ActivationFunctionType
+    queue = {"pe": g.tensor, "v": g.vector, "s": g.scalar, "y": g.sync, "g": g}
+
+    known = {q: {} for q in queue}
+    count, total = {q: 0 for q in queue}, {}
+    history = {}
+    ndma, serial = [0], [0]
+
+    def R(name, lo, hi, phase=None):
+        ap = T[name][:, lo:hi] if phase is None else T[name][:, lo + phase:hi:4]
+        return (ap, name, lo, hi, phase)
+
+    def order(q, reads, writes):
+        need = {}
+        for refs, w in ((reads, False), (writes, True)):
+            for (ap, name, lo, hi, ph) in refs:
+                for (l2, h2, p2, w2, call) in history.get(name, []):
+                    if (w or w2 or name[:4] == "bank") and lo < h2 and l2 < hi and (ph is None or p2 is None or ph == p2):
+                        need[call[0]] = call
+        for i in sorted(need, reverse=True):
+            call = need[i]
+            if known[q].get(call[1], 0) < call[2]:
+                queue[q].wait_ge(T.sem[call[1]], call[2])
+                for s, v in call[3].items():
+                    known[q][s] = max(known[q].get(s, 0), v)
+
+    def record(q, sem, val, reads, writes):
+        clock = dict(known[q]) if q else {}
+        clock[sem] = max(val, clock.get(sem, 0))
+        total[sem] = max(val, total.get(sem, 0))
+        serial[0] += 1
+        call = (serial[0], sem, val, clock)
+        for refs, w in ((reads, False), (writes, True)):
+            for (ap, name, lo, hi, ph) in refs:
+                history.setdefault(name, []).append((lo, hi, ph, w, call))
+
+    def do(q, fn, writes, reads):
+        order(q, reads, writes)
+        count[q] += 1
+        fn(queue[q]).then_inc(T.sem["c_" + q], 1)
+        record(q, "c_" + q, count[q], reads, writes)
+
+    def dma(q, out, in_, writes=(), reads=()):
+        order(q, reads, writes)
+        sem = "dma%d" % ndma[0]
+        ndma[0] += 1
+        queue[q].dma_start(out, in_).then_inc(T.sem[sem], 16)
+        record(q, sem, 16, reads, writes)
+
+    def mm(bank, n, st, mv):
+        out = R("bank%d" % bank, 0, n)
+        do("pe", lambda e: e.matmul_mx(out[0], st[0][0], st[1][0], mv[0][0], mv[1][0], True, True), [out], [st[0], st[1], mv[0], mv[1]])
+
+    def quant(c, s, t):
+        do("v", lambda e: e.quantize_mx(c[0], s[0], t[0]), [c, s], [t])
+
+    def ts(out, in0, s1, s2, op0, op1=None):
+        a1 = s1[0] if isinstance(s1, tuple) else s1
+        a2 = s2[0] if isinstance(s2, tuple) else s2
+        reads = [in0] + [s for s in (s1, s2) if isinstance(s, tuple)]
+        if op1 is None:
+            do("v", lambda e: e.tensor_scalar(out[0], in0[0], a1, None, op0), [out], reads)
+        else:
+            do("v", lambda e: e.tensor_scalar(out[0], in0[0], a1, a2, op0, op1), [out], reads)
+
+    def tt(out, a, b, op):
+        do("v", lambda e: e.tensor_tensor(out[0], a[0], b[0], op), [out], [a, b])
+
+    def scan(out, a, b, init, op0, op1):
+        i = init[0] if isinstance(init, tuple) else init
+        do("v", lambda e: e.tensor_tensor_scan(out[0], a[0], b[0], i, op0, op1), [out], [a, b] + ([init] if isinstance(init, tuple) else []))
+
+    def vcopy(out, in_):
+        do("v", lambda e: e.tensor_copy(out[0], in_[0]), [out], [in_])
+
+    def fill(out, val):
+        do("v", lambda e: e.memset(out[0], val), [out], [])
+
+    def act(out, in_, func, **kw):
+        do("s", lambda e: e.activation(out[0], in_[0], func, **kw), [out], [in_])
+
+    def pair(c, s, lo, hi):
+        return R(c, lo, hi), R(s, lo, hi)
+
+    dma("y", T.ut[:, 0:32], T.u[:, 0:32], [R("ut", 0, 32)])
+    dma("s", T.xt0[:, 0:4 * CA], T.x[:, 0:4 * CA], [R("xt0", 0, 4 * CA)])
+    dma("y", T.prow[0:1, :], T.p[:], [R("prow", 0, 8)])
+    dma("y", T.xt0[:, 4 * CA:4 * C], T.x[:, 4 * CA:4 * C], [R("xt0", 4 * CA, 4 * C)])
+    dma("y", T.cw[:, 0:512].bitcast(dt.uint8), T.wc[:, :], [R("cw", 0, 512)])
+    dma("s", T.sw[:, :], T.ws[:, :], [R("sw", 0, 512)])
+    dma("y", T.vt[:, :], T.v[:, :], [R("vt", 0, 512)])
+
+    eb = R("eb", 0, 516)
+    fill(eb, 0.0)
+    do("g", lambda e: e.affine_select(T.eb[:, :], T.eb[:, :], [[-1, 516]], A.not_equal, 2.0 ** -6, 3, 4), [eb], [eb])
+    do("g", lambda e: e.iota(T.mi[:, :], [[1, CA]], 128, -1), [R("mi", 0, CA)], [])
+    do("g", lambda e: e.iota(T.pid[:, :], [[0, 12]], 0, 1), [R("pid", 0, 12)], [])
+    do("g", lambda e: e.iota(T.kk[:, :], [[16, 12]], 0, 0, allow_small_or_imprecise_dtypes=True), [R("kk", 0, 12)], [])
+    fill(R("offz", 0, 8), 0)
+    fill(R("ut", 32, 512), 0.0)
+    fill(R("zero", 0, CA), 0.0)
+    fill(R("yA", 0, 1), BASE)
+    fill(R("yB", 0, 1), BASE)
+    for b in range(4):
+        quant(R("ce", 128 * b, 128 * b + 128), R("se", 128 * b, 128 * b + 128), R("eb", 3 - b, 515 - b))
+    quant(R("cu", 0, 128), R("su", 0, 128), R("ut", 0, 512))
+    do("v", lambda e: e.tensor_copy(T.cu0[:, 0:128].bitcast(dt.uint32), T.cu[:, 0:8].bitcast(dt.uint32).indirect(T.offz[:, 0:8])), [R("cu0", 0, 128)], [R("cu", 0, 8), R("offz", 0, 8)])
+    do("s", lambda e: e.activation(T.su0[:, 0:128], T.su[:, 0:8].indirect(T.offz[:, 0:8]), ACT.Copy), [R("su0", 0, 128)], [R("su", 0, 8), R("offz", 0, 8)])
+    prow, pf, pb = R("prow", 0, 8), R("pf", 0, 8), R("pb", 0, 8)
+    do("v", lambda e: e.tensor_scalar(T.pf[0:1, :], T.prow[0:1, :], TINY, None, A.mult), [pf], [prow])
+    do("g", lambda e: e.partition_broadcast(T.pb[:, :], T.pf[0:1, :], 128), [pb], [pf])
+    do("g", lambda e: e.affine_select(T.pb[:, :], T.pb[:, :], [[-16, 8]], A.is_ge, 0.0, 0, 1), [pb], [pb])
+    mi, mask = R("mi", 0, CA), R("mask", 0, CA)
+    pid, kk, kt = R("pid", 0, 12), R("kk", 0, 12), R("kt", 0, 12)
+    ts(mi, mi, 15, None, A.bitwise_and)
+    ts(mask, mi, 0.0, 512.0, A.is_gt, A.mult)
+
+    def constants1():
+        ts(R("hit", 0, 16), R("mi", 0, 16), 0.0, TINY, A.is_equal, A.mult)
+        ts(pid, pid, 15, None, A.bitwise_and)
+        scan(R("rs", 0, 16), R("mask", 0, 16), R("hit", 0, 16), 0.0, A.mult, A.add)
+        tt(kk, kk, pid, A.add)
+        do("v", lambda e: e.reciprocal(T.sc[:, :], T.rs[:, 15:16]), [R("sc", 0, 1)], [R("rs", 15, 16)])
+
+    def constants2():
+        do("v", lambda e: e.tensor_reduce(T.ps[:, :], T.pb[:, :], AxisListType.X, A.add), [R("ps", 0, 1)], [pb])
+        ts(kt, kk, 128.375, R("rs", 15, 16), A.add, A.mult)
+        vcopy(R("pp", 0, 1), R("ps", 0, 1))
+
+    dst = T.cores[(rank - 1) % N]
+    src = T.cores[(rank + 1) % N]
+    rid, pidn = topo.addr(dst)[0], topo.addr(dst)[1]
+    mine = topo.engines(core, dst)[:8]
+    theirs = topo.engines(src, core)[:8]
+    mask_out = sum(1 << e for e in mine)
+
+    def send(t):
+        c, s = pair("cx%d" % t, "sx%d" % t, 0, H)
+        order("g", [c, s], [])
+        rs, ls = T.sem["arr%d" % t], T.sem["left%d" % t]
+        g.remote_dma(out_ap=T["lc%d" % t][:, 0:H].bitcast(dt.uint8), in_ap=c[0].bitcast(dt.uint8), remote_sem=rs, local_sem=ls, pid=pidn, routing_id=rid, dma_engine_mask=mask_out)
+        g.remote_dma(out_ap=T["ls%d" % t][:, 0:H], in_ap=s[0], remote_sem=rs, local_sem=ls, pid=pidn, routing_id=rid, dma_engine_mask=mask_out)
+        total["left%d" % t] = 2 * len(mine)
+        record(None, "arr%d" % t, 2 * len(theirs), [], [R("lc%d" % t, 0, H), R("ls%d" % t, 0, H)])
+
+    def quant_x(t, c):
+        lo, hi = LO[c], LO[c] + NC[c]
+        quant(R("cx%d" % t, lo, hi), R("sx%d" % t, lo, hi), R("xt%d" % t, 4 * lo, 4 * hi))
+
+    def quant_z(t, c):
+        lo, hi = LO[c], LO[c] + NC[c]
+        quant(R("cz%d" % t, lo, hi), R("sz%d" % t, lo, hi), R("zt%d" % t, 4 * lo, 4 * hi))
+
+    def xcols(t, c):
+        return pair("cx%d" % t, "sx%d" % t, LO[c], LO[c] + NC[c])
+
+    def score(t, c, bank):
+        mm(bank, NC[c], pair("cu0", "su0", 0, 128), xcols(t, c))
+
+    def unpack(t, c, b, bank):
+        mm(bank, NC[c], pair("ce", "se", 128 * b, 128 * b + 128), xcols(t, c))
+
+    def cast(t, c, b, bank):
+        act(R("w%d%d" % (t % 2, b), LO[c], LO[c] + NC[c]), R("bank%d" % bank, 0, NC[c]), ACT.Copy)
+
+    def cast_own(t, c, b, bank):
+        act(R("n%d%d" % (t % 2, b), LO[c], LO[c] + NC[c]), R("bank%d" % bank, 0, NC[c]), ACT.Copy)
+
+    def unpack_far(t, b, bank):
+        mm(bank, H, pair("ce", "se", 128 * b, 128 * b + 128), pair("lc%d" % t, "ls%d" % t, 0, H))
+
+    def cast_far(t, b, bank):
+        act(R("w%d%d" % (t % 2, b), C, W), R("bank%d" % bank, 0, H), ACT.Copy)
+
+    def flags(t, c, bank):
+        lo, n = LO[c], NC[c]
+        ts(R("fl", lo, lo + n), R("bank%d" % bank, 0, n), 0.0, 11.0, A.is_gt, A.mult)
+
+    def chain(t, c):
+        lo, n = LO[c], NC[c]
+        hi = lo + n
+        y = "y" + c
+        first = t == 0 and c == "A"
+        fl, dy, ee, ae, d0, d1, pl, sm = [R(k, lo, hi) for k in ("fl", "dy", "ee", "ae", "d0", "d1", "pl", "sm")]
+        before = lo if c == "B" else C
+        pp, xi = R("pp", 0, 1), R("xi", 0, 1)
+        k0, k1 = lo // 16, hi // 16
+        o1 = R("o1", k0, k1)
+
+        def distance():
+            scan(ee, fl, dy, 0.0 if first else R("ee", before - 1, before), A.add, A.subtract)
+            act(ae, ee, ACT.Abs, scale=TINY)
+
+        return [
+            lambda: scan(R(y, 1, n + 1), fl, R("zero", 0, n), BASE if first else xi, A.add, A.add),
+            lambda: scan(dy, R(y, 1, n + 1), R(y, 0, n), 0.0, A.max, A.subtract),
+            distance,
+            lambda: ts(xi, R("ee", hi - 1, hi), BASE, None, A.add),
+            lambda: ts(d0, ae, pp, None, A.subtract),
+            lambda: ts(d1, ae, pp, None, A.add),
+            lambda: scan(pl, d0, d1, 128.0 * TINY if first else R("pl", before - 1, before), A.max, A.min),
+            lambda: scan(sm, R("mask", 0, n), pl, 0.0, A.mult, A.add),
+            lambda: do("v", lambda e: e.tensor_tensor(o1[0], T.kt[:, 0:n // 16], T.sm[:, lo + 15:hi:16], A.subtract), [o1], [R("kt", 0, n // 16), sm]),
+            lambda: ts(R("off%d" % t, k0, k1), o1, R("sc", 0, 1), None, A.mult),
+        ]
+
+    def window(t, c, b):
+        a, e = (0, C) if c == "A" else (CA, W)
+        return R("w%d%d" % (t % 2, b), a, e), R("off%d" % t, LO[c] // 16, (LO[c] + NC[c]) // 16)
+
+    def zpiece(t, c, b):
+        return R("zt%d" % t, 4 * LO[c], 4 * (LO[c] + NC[c]), b)
+
+    def gather_add(t, c, b):
+        w, off = window(t, c, b)
+        own = R("n%d%d" % (t % 2, b), LO[c], LO[c] + NC[c])
+        z = zpiece(t, c, b)
+        do("v", lambda e: e.tensor_tensor(z[0], w[0].indirect(off[0]), own[0], A.add), [z], [w, off, own])
+
+    def gather(t, c, b):
+        w, off = window(t, c, b)
+        f = R("f%d%d" % (t % 2, b), LO[c], LO[c] + NC[c])
+        do("s", lambda e: e.activation(f[0], w[0].indirect(off[0]), ACT.Copy), [f], [w, off])
+
+    def add(t, c, b, bank):
+        tt(zpiece(t, c, b), R("bank%d" % bank, 0, NC[c]), R("f%d%d" % (t % 2, b), LO[c], LO[c] + NC[c]), A.add)
+
+    def layer(t, c, b, bank):
+        mm(bank, NC[c], pair("cw", "sw", 128 * b, 128 * b + 128), pair("cz%d" % t, "sz%d" % t, LO[c], LO[c] + NC[c]))
+
+    def renew(t, c, b, bank):
+        lo, hi = 4 * LO[c], 4 * (LO[c] + NC[c])
+        tt(R("xt%d" % (t + 1), lo, hi, b), R("bank%d" % bank, 0, NC[c]), R("xt%d" % t, lo, hi, b), A.add)
+
+    HA, HB, R0, R1, M, S = (0, 1), (2, 3), 4, 5, 6, 7
+    DA = [M, M, HA[0], HA[1]]
+    DB = [M, R1, HB[0], HB[1]]
+
+    quant_x(0, "A")
+    send(0)
+    score(0, "A", R0)
+    constants1()
+    flags(0, "A", R0)
+    for b in (0, 2, 3):
+        unpack(0, "A", b, DA[b])
+        cast(0, "A", b, DA[b])
+        if b == 0:
+            cast_own(0, "A", b, DA[b])
+    ca = chain(0, "A")
+    ca[0]()
+    constants2()
+    ca[1]()
+    quant_x(0, "B")
+    for i in (2, 3, 4, 5, 6):
+        ca[i]()
+
+    for t in range(ROUNDS):
+        last = t == ROUNDS - 1
+        unpack(t, "A", 1, DA[1])
+        cast(t, "A", 1, DA[1])
+        cast_own(t, "A", 1, DA[1])
+        for b in (1, 0):
+            unpack(t, "B", b, DB[b])
+            cast(t, "B", b, DB[b])
+        score(t, "B", S)
+        for b in (2, 3):
+            unpack(t, "B", b, DB[b])
+            cast(t, "B", b, DB[b])
+        for i in (7, 8, 9):
+            ca[i]()
+        cb = chain(t, "B")
+        gather_add(t, "A", 1)
+        for b in (2, 3):
+            gather(t, "A", b)
+        for b in (1, 0):
+            cast_own(t, "B", b, DB[b])
+        flags(t, "B", S)
+        gather_add(t, "A", 0)
+        cb[0]()
+        for b in (2, 3):
+            add(t, "A", b, DA[b])
+            cb[b - 1]()
+        quant_z(t, "A")
+        ra = (R0, R1, HA[0], HA[1])
+        for b in range(4):
+            layer(t, "A", b, ra[b])
+        for i in (3, 4, 5):
+            cb[i]()
+        for b in range(4):
+            renew(t, "A", b, ra[b])
+            cb[6 + b]()
+        quant_x(t + 1, "A")
+        tf = (M, S, HA[0], HA[1])
+        for b in range(4):
+            unpack_far(t, b, tf[b])
+            cast_far(t, b, tf[b])
+        if not last:
+            send(t + 1)
+            score(t + 1, "A", R0)
+            ca = chain(t + 1, "A")
+        else:
+            quant(R("cv", 0, 128), R("sv", 0, 128), R("vt", 0, 512))
+            mm(R0, CA, pair("cv", "sv", 0, 128), xcols(ROUNDS, "A"))
+        gather_add(t, "B", 0)
+        for b in (2, 3):
+            gather(t, "B", b)
+        if not last:
+            flags(t + 1, "A", R0)
+        gather_add(t, "B", 1)
+        if not last:
+            ca[0]()
+        for b in (2, 3):
+            add(t, "B", b, DB[b])
+            if not last:
+                ca[b - 1]()
+        quant_z(t, "B")
+        if not last:
+            for b in (0, 2, 3):
+                unpack(t + 1, "A", b, DA[b])
+        rb = (R1, HB[0], HB[1], S)
+        for b in range(4):
+            layer(t, "B", b, rb[b])
+        if not last:
+            for i in (3, 4, 5):
+                ca[i]()
+            for b in (0, 2, 3):
+                cast(t + 1, "A", b, DA[b])
+                if b == 0:
+                    cast_own(t + 1, "A", b, DA[b])
+        else:
+            act(R("yo", 0, CA), R("bank%d" % R0, 0, CA), ACT.Copy)
+            act(R("aof", 0, C), R("pl", 0, C), ACT.Identity, scale=-1.0 / TINY, bias=128.0)
+        for b in range(4):
+            renew(t, "B", b, rb[b])
+            if not last and b == 0:
+                ca[6]()
+        quant_x(t + 1, "B")
+
+    xc, xs = "cx%d" % ROUNDS, "sx%d" % ROUNDS
+    mm(M, CB, pair("cv", "sv", 0, 128), xcols(ROUNDS, "B"))
+    dma("y", T.oc[:, 0:4 * CA], T[xc][:, 0:CA].bitcast(dt.uint8), [], [R(xc, 0, CA)])
+    dma("y", T.y[:, 0:CA], T.yo[:, 0:CA], [], [R("yo", 0, CA)])
+    dma("y", T.ao[:, :], T.aof[0:128:16, :], [], [R("aof", 0, C)])
+    vcopy(R("yo", CA, C), R("bank%d" % M, 0, CB))
+    dma("y", T.oc[:, 4 * CA:4 * C], T[xc][:, CA:C].bitcast(dt.uint8), [], [R(xc, CA, C)])
+    for k in range(4):
+        dma("sysy"[k], T.osc[4 * k:4 * k + 4, :], T[xs][32 * k:32 * k + 4, :], [], [R(xs, 0, C)])
+    dma("s", T.y[:, CA:C], T.yo[:, CA:C], [], [R("yo", CA, C)])
+    for s in sorted(total):
+        if s[:3] != "arr":
+            g.wait_ge(T.sem[s], total[s])

@@ -1,10 +1,30 @@
-from concourse.mybir import dt, AluOpType, ActivationFunctionType, AxisListType
+from concourse.mybir import dt, AluOpType, ActivationFunctionType
+
+ORDER = """
+mi0 ldp zo ldu ldx0 ldx1 zz ldx2 ldv ldw mi1 eb0 yA0 eb1 ma0 hi0 ma1 yB0 zu ma2 hi1 pf pb0 eq0 qu pb1 rs eq1 kk0 ps eq3 pp u1 qs
+u0 snd0 lds ma3 ma4 hi2 qx0A ic sc0A eq2 un0A0 fl0A un0A2 ca0A0 ch0A0 qx0B un0A3 ca0A2 ch0A1 sc0B ow0A0 ch0A2 kt un0B1 ab0A si
+fl0B un0A1 ca0B1 ch0A5 un0B2 ch0A3 ch0A4 ca0A1 un0B3 ch0A6 ca0B2 ch0B0 ch0A7 ow0A1 ca0B3 ch0B1 ch0A8 un0B0 qv ca0A3 ch0A9 ch0B2
+ca0B0 ga0A1 gs0A3 ga0A0 gs0A2 ad0A3 ch0B3 ow0B1 ad0A2 ab0B qz0A ch0B5 ow0B0 ch0B4 la0A3 ch0B6 ch0B7 la0A1 re0A3 la0A2 ch0B8 re0A1
+la0A0 re0A2 re0A0 ch0B9 qx1A snd1 uf00 uf01 cf00 uf03 cf01 ga0B0 uf02 cf03 sc1A ga0B1 cf02 gs0B3 un1A3 fl1A gs0B2 un1A0 ad0B3 ch1A0
+un1A2 ca1A0 ad0B2 ca1A3 qz0B ch1A1 ow1A0 la0B3 ch1A2 ca1A2 la0B1 re0B3 la0B2 ab1A re0B1 la0B0 re0B2 un1A1 re0B0 ch1A5 ca1A1 qx1B
+ch1A4 ch1A3 sc1B ow1A1 ch1A6 un1B3 ch1A7 un1B1 fl1B ca1B3 un1B2 ch1A8 ca1B1 ch1B0 un1B0 ch1A9 ca1B2 ch1B1 ga1A1 gs1A3 ch1B2 ca1B0
+ad1A3 gs1A2 ga1A0 ow1B0 ad1A2 ab1B uf10 ch1B5 uf11 qz1A ch1B3 ow1B1 ch1B4 la1A3 cf10 ch1B6 cf11 ch1B7 la1A2 re1A3 la1A1 ch1B8 re1A2
+la1A0 re1A1 uf12 re1A0 uf13 cf12 ch1B9 qx2A cf13 gs1B2 ga1B1 un2A2 snd2 gs1B3 ga1B0 sc2A ca2A2 ad1B2 un2A3 ad1B3 un2A0 fl2A qz1B
+ca2A0 ch2A0 la1B2 ow2A0 ch2A1 la1B0 re1B2 la1B3 ch2A2 re1B0 la1B1 ab2A re1B3 un2A1 ch2A3 re1B1 ch2A4 ca2A1 qx2B ch2A5 ow2A1 sc2B
+ch2A6 un2B2 ca2A3 fl2B un2B0 ch2A7 ca2B2 ch2B0 un2B3 ch2A8 ca2B0 ch2B1 un2B1 ch2A9 ca2B3 ch2B2 ga2A0 ca2B1 gs2A2 ga2A1 gs2A3 ad2A2
+ab2B ad2A3 ch2B5 ch2B4 qz2A ow2B0 ch2B6 ow2B1 uf21 ch2B7 ea la2A3 ch2B8 la2A2 cf21 re2A3 uf20 ch2B9 re2A2 uf23 cf20 ga2B1 la2A1 cf23
+ga2B0 uf22 gs2B3 la2A0 re2A1 cf22 re2A0 gs2B2 ad2B3 qx3A ad2B2 yA oA oa qz2B eA la2B0 la2B3 oy re2B0 la2B1 re2B3 la2B2 re2B1 re2B2
+qx3B yB oB os0 os3 os2 os1 eB oz
+"""
+GV = {"A": (0, 1), "B": (0, 1)}
+BANKS = {}
 
 N = 8
 CA, CB, C, H, W = 192, 128, 320, 128, 448
 LO = {"A": 0, "B": CA}
 NC = {"A": CA, "B": CB}
 ROUNDS = 3
+ENGINES = slice(0, 8)
 TINY = 2.0 ** -30
 BASE = 49152.0
 
@@ -15,14 +35,15 @@ SCRATCH = {
     "cu0": ("sbuf", [128, 128], X4), "su0": ("sbuf", [128, 128], U8),
     "cv": ("sbuf", [128, 128], X4), "sv": ("sbuf", [128, 128], U8),
     "cw": ("sbuf", [128, 512], X4), "sw": ("sbuf", [128, 512], U8),
+    "cq": ("sbuf", [128, H], X4), "sq": ("sbuf", [128, H], U8),
     "eb": ("sbuf", [128, 516], B16), "ce": ("sbuf", [128, 512], X4), "se": ("sbuf", [128, 512], U8),
     "offz": ("sbuf", [128, 8], U16), "zero": ("sbuf", [128, CA], B16),
-    "mi": ("sbuf", [128, CA], I32), "mask": ("sbuf", [128, CA], B16), "hit": ("sbuf", [128, 16], B16),
-    "rs": ("sbuf", [128, 16], F32), "sc": ("sbuf", [128, 1], F32),
-    "pid": ("sbuf", [128, 12], I32), "kk": ("sbuf", [128, 12], F32), "kt": ("sbuf", [128, 12], F32),
-    "prow": ("sbuf", [1, 8], I32), "pf": ("sbuf", [1, 8], F32), "pb": ("sbuf", [128, 8], F32),
-    "ps": ("sbuf", [128, 1], F32), "pp": ("sbuf", [128, 1], B16),
-    "xi": ("sbuf", [128, 1], F32),
+    "mi": ("sbuf", [128, 16], I32), "mask": ("sbuf", [128, CA], B16), "hit": ("sbuf", [128, 16], B16),
+    "mask2": ("sbuf", [128, 16], B16), "hit2": ("sbuf", [128, 16], B16),
+    "rs": ("sbuf", [128, 16], F32), "si": ("sbuf", [128, 16], F32), "ic": ("sbuf", [128, 1], F32),
+    "kk": ("sbuf", [128, 12], F32), "kt": ("sbuf", [128, 12], F32),
+    "prow": ("sbuf", [1, 8], I32), "pf": ("sbuf", [1, 8], F32), "pb": ("sbuf", [128, 8], F32), "pj": ("sbuf", [128, 8], F32),
+    "ps": ("sbuf", [128, 1], F32), "pp": ("sbuf", [128, 1], B16), "xi": ("sbuf", [128, 1], F32),
     "fl": ("sbuf", [128, C], B16), "yA": ("sbuf", [128, CA + 8], B16), "yB": ("sbuf", [128, CB + 8], B16),
     "dy": ("sbuf", [128, C], B16), "ee": ("sbuf", [128, C], B16), "ae": ("sbuf", [128, C], B16),
     "d0": ("sbuf", [128, C], B16), "d1": ("sbuf", [128, C], B16), "pl": ("sbuf", [128, C], B16),
@@ -43,24 +64,33 @@ for _t in range(ROUNDS):
 for _t in range(2):
     for _b in range(4):
         SCRATCH["w%d%d" % (_t, _b)] = ("sbuf", [128, W], B16)
-        SCRATCH["fn"[_b < 2] + "%d%d" % (_t, _b)] = ("sbuf", [128, C], B16)
+        SCRATCH["f%d%d" % (_t, _b)] = ("sbuf", [128, C], B16)
+        SCRATCH["n%d%d" % (_t, _b)] = ("sbuf", [128, C], B16)
 for _b in range(8):
     SCRATCH["bank%d" % _b] = ("psum", [128, 512], F32)
-NDMA = 18
+NDMA = 17
 SEMAPHORES = ["c_pe", "c_v", "c_s", "c_g"] + ["dma%d" % _i for _i in range(NDMA)] + ["arr%d" % _t for _t in range(ROUNDS)] + ["left%d" % _t for _t in range(ROUNDS)]
 
 
 def rank_program(g, core, T, topo):
+    if T.rank_of(core) is not None:
+        build(g, core, T, topo, True)
+
+
+def build(g, core, T, topo, issue):
     rank = T.rank_of(core)
-    if rank is None:
-        return
     A, ACT = AluOpType, ActivationFunctionType
     queue = {"pe": g.tensor, "v": g.vector, "s": g.scalar, "y": g.sync, "g": g}
+    dst, src = T.cores[(rank - 1) % N], T.cores[(rank + 1) % N]
+    rid, pidn = topo.addr(dst)[0], topo.addr(dst)[1]
+    mine, theirs = topo.engines(core, dst)[ENGINES], topo.engines(src, core)[ENGINES]
+    mask_out = sum(1 << e for e in mine)
 
     known = {q: {} for q in queue}
     count, total = {q: 0 for q in queue}, {}
     history = {}
     ndma, serial = [0], [0]
+    calls, taken = [], {}
 
     def R(name, lo, hi, phase=None):
         ap = T[name][:, lo:hi] if phase is None else T[name][:, lo + phase:hi:4]
@@ -90,175 +120,181 @@ def rank_program(g, core, T, topo):
             for (ap, name, lo, hi, ph) in refs:
                 history.setdefault(name, []).append((lo, hi, ph, w, call))
 
-    def do(q, fn, writes, reads):
+    def put(name, q, kind, fn, writes, reads):
+        calls.append((name, q, kind, fn, writes, reads))
+
+    def do(name, q, fn, writes, reads):
+        put(name, q, "c", fn, writes, reads)
+
+    def dma(name, q, out, in_, writes=(), reads=()):
+        put(name, q, "d", lambda e: e.dma_start(out, in_), writes, reads)
+
+    def start(call):
+        name, q, kind, fn, writes, reads = call
         order(q, reads, writes)
-        count[q] += 1
-        fn(queue[q]).then_inc(T.sem["c_" + q], 1)
-        record(q, "c_" + q, count[q], reads, writes)
+        if kind == "c":
+            count[q] += 1
+            fn(queue[q]).then_inc(T.sem["c_" + q], 1)
+            record(q, "c_" + q, count[q], reads, writes)
+        elif kind == "d":
+            sem = "dma%d" % ndma[0]
+            ndma[0] += 1
+            fn(queue[q]).then_inc(T.sem[sem], 16)
+            record(q, sem, 16, reads, writes)
+        else:
+            fn(queue[q])
+            total["left" + kind] = 2 * len(mine)
+            record(None, "arr" + kind, 2 * len(theirs), [], writes)
 
-    def dma(q, out, in_, writes=(), reads=()):
-        order(q, reads, writes)
-        sem = "dma%d" % ndma[0]
-        ndma[0] += 1
-        queue[q].dma_start(out, in_).then_inc(T.sem[sem], 16)
-        record(q, sem, 16, reads, writes)
+    def B(use, n):
+        return R("bank%d" % BANKS.get(use, taken.get(use)), 0, n)
 
-    def mm(bank, n, st, mv):
-        out = R("bank%d" % bank, 0, n)
-        do("pe", lambda e: e.matmul_mx(out[0], st[0][0], st[1][0], mv[0][0], mv[1][0], True, True), [out], [st[0], st[1], mv[0], mv[1]])
+    def mm(name, bank, n, st, mv):
+        taken[name] = bank
+        out = B(name, n)
+        do(name, "pe", lambda e: e.matmul_mx(out[0], st[0][0], st[1][0], mv[0][0], mv[1][0], True, True), [out], [st[0], st[1], mv[0], mv[1]])
 
-    def quant(c, s, t):
-        do("v", lambda e: e.quantize_mx(c[0], s[0], t[0]), [c, s], [t])
+    def quant(name, c, s, t):
+        do(name, "v", lambda e: e.quantize_mx(c[0], s[0], t[0]), [c, s], [t])
 
-    def ts(out, in0, s1, s2, op0, op1=None):
+    def ts(name, out, in0, s1, s2, op0, op1=None):
         a1 = s1[0] if isinstance(s1, tuple) else s1
         a2 = s2[0] if isinstance(s2, tuple) else s2
         reads = [in0] + [s for s in (s1, s2) if isinstance(s, tuple)]
         if op1 is None:
-            do("v", lambda e: e.tensor_scalar(out[0], in0[0], a1, None, op0), [out], reads)
+            do(name, "v", lambda e: e.tensor_scalar(out[0], in0[0], a1, None, op0), [out], reads)
         else:
-            do("v", lambda e: e.tensor_scalar(out[0], in0[0], a1, a2, op0, op1), [out], reads)
+            do(name, "v", lambda e: e.tensor_scalar(out[0], in0[0], a1, a2, op0, op1), [out], reads)
 
-    def tt(out, a, b, op):
-        do("v", lambda e: e.tensor_tensor(out[0], a[0], b[0], op), [out], [a, b])
+    def tt(name, out, a, b, op):
+        do(name, "v", lambda e: e.tensor_tensor(out[0], a[0], b[0], op), [out], [a, b])
 
-    def scan(out, a, b, init, op0, op1):
+    def scan(name, out, a, b, init, op0, op1):
         i = init[0] if isinstance(init, tuple) else init
-        do("v", lambda e: e.tensor_tensor_scan(out[0], a[0], b[0], i, op0, op1), [out], [a, b] + ([init] if isinstance(init, tuple) else []))
+        do(name, "v", lambda e: e.tensor_tensor_scan(out[0], a[0], b[0], i, op0, op1), [out], [a, b] + ([init] if isinstance(init, tuple) else []))
 
-    def vcopy(out, in_):
-        do("v", lambda e: e.tensor_copy(out[0], in_[0]), [out], [in_])
+    def fill(name, out, val):
+        do(name, "v", lambda e: e.memset(out[0], val), [out], [])
 
-    def fill(out, val):
-        do("v", lambda e: e.memset(out[0], val), [out], [])
-
-    def act(out, in_, func, **kw):
-        do("s", lambda e: e.activation(out[0], in_[0], func, **kw), [out], [in_])
+    def act(name, out, in_, func, **kw):
+        do(name, "s", lambda e: e.activation(out[0], in_[0], func, **kw), [out], [in_])
 
     def pair(c, s, lo, hi):
         return R(c, lo, hi), R(s, lo, hi)
 
-    dma("y", T.ut[:, 0:32], T.u[:, 0:32], [R("ut", 0, 32)])
-    dma("s", T.xt0[:, 0:4 * CA], T.x[:, 0:4 * CA], [R("xt0", 0, 4 * CA)])
-    dma("y", T.prow[0:1, :], T.p[:], [R("prow", 0, 8)])
-    dma("y", T.xt0[:, 4 * CA:4 * C], T.x[:, 4 * CA:4 * C], [R("xt0", 4 * CA, 4 * C)])
-    dma("y", T.cw[:, 0:512].bitcast(dt.uint8), T.wc[:, :], [R("cw", 0, 512)])
-    dma("s", T.sw[:, :], T.ws[:, :], [R("sw", 0, 512)])
-    dma("y", T.vt[:, :], T.v[:, :], [R("vt", 0, 512)])
+    dma("ldx0", "y", T.xt0[:, 0:4 * H], T.x[:, 0:4 * H], [R("xt0", 0, 4 * H)])
+    dma("ldu", "s", T.ut[:, 0:32], T.u[:, 0:32], [R("ut", 0, 32)])
+    dma("ldp", "y", T.prow[0:1, :], T.p[:], [R("prow", 0, 8)])
+    dma("ldx1", "s", T.xt0[:, 4 * H:4 * CA], T.x[:, 4 * H:4 * CA], [R("xt0", 4 * H, 4 * CA)])
+    dma("ldx2", "y", T.xt0[:, 4 * CA:4 * C], T.x[:, 4 * CA:4 * C], [R("xt0", 4 * CA, 4 * C)])
+    dma("ldw", "y", T.cw[:, 0:512].bitcast(dt.uint8), T.wc[:, :], [R("cw", 0, 512)])
+    dma("lds", "s", T.sw[:, :], T.ws[:, :], [R("sw", 0, 512)])
+    dma("ldv", "y", T.vt[:, :], T.v[:, :], [R("vt", 0, 512)])
 
-    eb = R("eb", 0, 516)
-    fill(eb, 0.0)
-    do("g", lambda e: e.affine_select(T.eb[:, :], T.eb[:, :], [[-1, 516]], A.not_equal, 2.0 ** -6, 3, 4), [eb], [eb])
-    do("g", lambda e: e.iota(T.mi[:, :], [[1, CA]], 128, -1), [R("mi", 0, CA)], [])
-    do("g", lambda e: e.iota(T.pid[:, :], [[0, 12]], 0, 1), [R("pid", 0, 12)], [])
-    do("g", lambda e: e.iota(T.kk[:, :], [[16, 12]], 0, 0, allow_small_or_imprecise_dtypes=True), [R("kk", 0, 12)], [])
-    fill(R("offz", 0, 8), 0)
-    fill(R("ut", 32, 512), 0.0)
-    fill(R("zero", 0, CA), 0.0)
-    fill(R("yA", 0, 1), BASE)
-    fill(R("yB", 0, 1), BASE)
+    eb, mi, pb = R("eb", 0, 516), R("mi", 0, 16), R("pb", 0, 8)
+    fill("eb0", eb, 0.0)
+    do("mi0", "g", lambda e: e.iota(T.mi[:, :], [[-1, 16]], 16, 1), [mi], [])
+    do("eb1", "g", lambda e: e.affine_select(T.eb[:, :], T.eb[:, :], [[-1, 516]], A.not_equal, 2.0 ** -6, 3, 4), [eb], [eb])
+    do("kk0", "g", lambda e: e.iota(T.kk[:, :], [[16, 12]], 128, 0, allow_small_or_imprecise_dtypes=True), [R("kk", 0, 12)], [])
+    fill("zo", R("offz", 0, 8), 0)
+    fill("zu", R("ut", 32, 512), 0.0)
+    fill("zz", R("zero", 0, CA), 0.0)
+    fill("yA0", R("yA", 0, 1), BASE)
+    fill("yB0", R("yB", 0, 1), BASE)
     for b in range(4):
-        quant(R("ce", 128 * b, 128 * b + 128), R("se", 128 * b, 128 * b + 128), R("eb", 3 - b, 515 - b))
-    quant(R("cu", 0, 128), R("su", 0, 128), R("ut", 0, 512))
-    do("v", lambda e: e.tensor_copy(T.cu0[:, 0:128].bitcast(dt.uint32), T.cu[:, 0:8].bitcast(dt.uint32).indirect(T.offz[:, 0:8])), [R("cu0", 0, 128)], [R("cu", 0, 8), R("offz", 0, 8)])
-    do("s", lambda e: e.activation(T.su0[:, 0:128], T.su[:, 0:8].indirect(T.offz[:, 0:8]), ACT.Copy), [R("su0", 0, 128)], [R("su", 0, 8), R("offz", 0, 8)])
-    prow, pf, pb = R("prow", 0, 8), R("pf", 0, 8), R("pb", 0, 8)
-    do("v", lambda e: e.tensor_scalar(T.pf[0:1, :], T.prow[0:1, :], TINY, None, A.mult), [pf], [prow])
-    do("g", lambda e: e.partition_broadcast(T.pb[:, :], T.pf[0:1, :], 128), [pb], [pf])
-    do("g", lambda e: e.affine_select(T.pb[:, :], T.pb[:, :], [[-16, 8]], A.is_ge, 0.0, 0, 1), [pb], [pb])
-    mi, mask = R("mi", 0, CA), R("mask", 0, CA)
-    pid, kk, kt = R("pid", 0, 12), R("kk", 0, 12), R("kt", 0, 12)
-    ts(mi, mi, 15, None, A.bitwise_and)
-    ts(mask, mi, 0.0, 512.0, A.is_gt, A.mult)
-
-    def constants1():
-        ts(R("hit", 0, 16), R("mi", 0, 16), 0.0, TINY, A.is_equal, A.mult)
-        ts(pid, pid, 15, None, A.bitwise_and)
-        scan(R("rs", 0, 16), R("mask", 0, 16), R("hit", 0, 16), 0.0, A.mult, A.add)
-        tt(kk, kk, pid, A.add)
-        do("v", lambda e: e.reciprocal(T.sc[:, :], T.rs[:, 15:16]), [R("sc", 0, 1)], [R("rs", 15, 16)])
-
-    def constants2():
-        do("v", lambda e: e.tensor_reduce(T.ps[:, :], T.pb[:, :], AxisListType.X, A.add), [R("ps", 0, 1)], [pb])
-        ts(kt, kk, 128.375, R("rs", 15, 16), A.add, A.mult)
-        vcopy(R("pp", 0, 1), R("ps", 0, 1))
-
-    dst = T.cores[(rank - 1) % N]
-    src = T.cores[(rank + 1) % N]
-    rid, pidn = topo.addr(dst)[0], topo.addr(dst)[1]
-    mine = topo.engines(core, dst)[:8]
-    theirs = topo.engines(src, core)[:8]
-    mask_out = sum(1 << e for e in mine)
+        quant("eq%d" % b, R("ce", 128 * b, 128 * b + 128), R("se", 128 * b, 128 * b + 128), R("eb", 3 - b, 515 - b))
+    quant("qu", R("cu", 0, 128), R("su", 0, 128), R("ut", 0, 512))
+    do("u0", "v", lambda e: e.tensor_copy(T.cu0[:, 0:128].bitcast(dt.uint32), T.cu[:, 0:8].bitcast(dt.uint32).indirect(T.offz[:, 0:8])), [R("cu0", 0, 128)], [R("cu", 0, 8), R("offz", 0, 8)])
+    do("u1", "s", lambda e: e.activation(T.su0[:, 0:128], T.su[:, 0:8].indirect(T.offz[:, 0:8]), ACT.Copy), [R("su0", 0, 128)], [R("su", 0, 8), R("offz", 0, 8)])
+    ts("mi1", mi, mi, 15, None, A.bitwise_and)
+    ts("ma0", R("mask", 0, 16), mi, 0.0, 512.0, A.is_gt, A.mult)
+    for k, (lo, hi, n) in enumerate(((16, 32, 16), (32, 64, 32), (64, 128, 64), (128, CA, CA - 128))):
+        act("ma%d" % (k + 1), R("mask", lo, hi), R("mask", 0, n), ACT.Copy)
+    ts("hi0", R("hit", 0, 16), mi, 0.0, TINY, A.is_equal, A.mult)
+    act("hi1", R("hit2", 0, 16), R("hit", 0, 16), ACT.Copy, scale=2.0 ** 60)
+    act("hi2", R("mask2", 0, 16), R("mask", 0, 16), ACT.Copy, scale=2.0 ** -18)
+    scan("rs", R("rs", 0, 16), R("mask", 0, 16), R("hit", 0, 16), 0.0, A.mult, A.add)
+    scan("si", R("si", 0, 16), R("mask2", 0, 16), R("hit2", 0, 16), 0.0, A.mult, A.add)
+    ts("ic", R("ic", 0, 1), R("mi", 0, 1), 0.375, None, A.add)
+    ts("kt", R("kt", 0, 12), R("kk", 0, 12), R("ic", 0, 1), R("rs", 15, 16), A.add, A.mult)
+    do("pf", "v", lambda e: e.tensor_scalar(T.pf[0:1, :], T.prow[0:1, :], TINY, None, A.mult), [R("pf", 0, 8)], [R("prow", 0, 8)])
+    do("pb0", "g", lambda e: e.partition_broadcast(T.pb[:, :], T.pf[0:1, :], 128), [pb], [R("pf", 0, 8)])
+    do("pb1", "g", lambda e: e.affine_select(T.pb[:, :], T.pb[:, :], [[-16, 8]], A.is_ge, 0.0, 0, 1), [pb], [pb])
+    do("ps", "s", lambda e: e.activation(T.pj[:, :], T.pb[:, :], ACT.Copy, accum_out=T.ps[:, :]), [R("pj", 0, 8), R("ps", 0, 1)], [pb])
+    act("pp", R("pp", 0, 1), R("ps", 0, 1), ACT.Copy)
 
     def send(t):
-        c, s = pair("cx%d" % t, "sx%d" % t, 0, H)
-        order("g", [c, s], [])
+        c, s = pair("cx%d" % t, "sx%d" % t, 0, H) if t else pair("cq", "sq", 0, H)
         rs, ls = T.sem["arr%d" % t], T.sem["left%d" % t]
-        g.remote_dma(out_ap=T["lc%d" % t][:, 0:H].bitcast(dt.uint8), in_ap=c[0].bitcast(dt.uint8), remote_sem=rs, local_sem=ls, pid=pidn, routing_id=rid, dma_engine_mask=mask_out)
-        g.remote_dma(out_ap=T["ls%d" % t][:, 0:H], in_ap=s[0], remote_sem=rs, local_sem=ls, pid=pidn, routing_id=rid, dma_engine_mask=mask_out)
-        total["left%d" % t] = 2 * len(mine)
-        record(None, "arr%d" % t, 2 * len(theirs), [], [R("lc%d" % t, 0, H), R("ls%d" % t, 0, H)])
+
+        def write(e):
+            e.remote_dma(out_ap=T["lc%d" % t][:, 0:H].bitcast(dt.uint8), in_ap=c[0].bitcast(dt.uint8), remote_sem=rs, local_sem=ls, pid=pidn, routing_id=rid, dma_engine_mask=mask_out)
+            e.remote_dma(out_ap=T["ls%d" % t][:, 0:H], in_ap=s[0], remote_sem=rs, local_sem=ls, pid=pidn, routing_id=rid, dma_engine_mask=mask_out)
+        put("snd%d" % t, "g", "%d" % t, write, [R("lc%d" % t, 0, H), R("ls%d" % t, 0, H)], [c, s])
 
     def quant_x(t, c):
         lo, hi = LO[c], LO[c] + NC[c]
-        quant(R("cx%d" % t, lo, hi), R("sx%d" % t, lo, hi), R("xt%d" % t, 4 * lo, 4 * hi))
+        quant("qx%d%s" % (t, c), R("cx%d" % t, lo, hi), R("sx%d" % t, lo, hi), R("xt%d" % t, 4 * lo, 4 * hi))
 
     def quant_z(t, c):
         lo, hi = LO[c], LO[c] + NC[c]
-        quant(R("cz%d" % t, lo, hi), R("sz%d" % t, lo, hi), R("zt%d" % t, 4 * lo, 4 * hi))
+        quant("qz%d%s" % (t, c), R("cz%d" % t, lo, hi), R("sz%d" % t, lo, hi), R("zt%d" % t, 4 * lo, 4 * hi))
 
     def xcols(t, c):
         return pair("cx%d" % t, "sx%d" % t, LO[c], LO[c] + NC[c])
 
     def score(t, c, bank):
-        mm(bank, NC[c], pair("cu0", "su0", 0, 128), xcols(t, c))
+        mm("sc%d%s" % (t, c), bank, NC[c], pair("cu0", "su0", 0, 128), xcols(t, c))
 
     def unpack(t, c, b, bank):
-        mm(bank, NC[c], pair("ce", "se", 128 * b, 128 * b + 128), xcols(t, c))
+        mm("un%d%s%d" % (t, c, b), bank, NC[c], pair("ce", "se", 128 * b, 128 * b + 128), xcols(t, c))
 
-    def cast(t, c, b, bank):
-        act(R("w%d%d" % (t % 2, b), LO[c], LO[c] + NC[c]), R("bank%d" % bank, 0, NC[c]), ACT.Copy)
+    def cast(t, c, b):
+        act("ca%d%s%d" % (t, c, b), R("w%d%d" % (t % 2, b), LO[c], LO[c] + NC[c]), B("un%d%s%d" % (t, c, b), NC[c]), ACT.Copy)
 
-    def cast_own(t, c, b, bank):
-        act(R("n%d%d" % (t % 2, b), LO[c], LO[c] + NC[c]), R("bank%d" % bank, 0, NC[c]), ACT.Copy)
+    def cast_own(t, c, b):
+        if b in GV[c]:
+            act("ow%d%s%d" % (t, c, b), R("n%d%d" % (t % 2, b), LO[c], LO[c] + NC[c]), B("un%d%s%d" % (t, c, b), NC[c]), ACT.Copy)
 
     def unpack_far(t, b, bank):
-        mm(bank, H, pair("ce", "se", 128 * b, 128 * b + 128), pair("lc%d" % t, "ls%d" % t, 0, H))
+        mm("uf%d%d" % (t, b), bank, H, pair("ce", "se", 128 * b, 128 * b + 128), pair("lc%d" % t, "ls%d" % t, 0, H))
 
-    def cast_far(t, b, bank):
-        act(R("w%d%d" % (t % 2, b), C, W), R("bank%d" % bank, 0, H), ACT.Copy)
+    def cast_far(t, b):
+        act("cf%d%d" % (t, b), R("w%d%d" % (t % 2, b), C, W), B("uf%d%d" % (t, b), H), ACT.Copy)
 
-    def flags(t, c, bank):
+    def flags(t, c):
         lo, n = LO[c], NC[c]
-        ts(R("fl", lo, lo + n), R("bank%d" % bank, 0, n), 0.0, 11.0, A.is_gt, A.mult)
+        ts("fl%d%s" % (t, c), R("fl", lo, lo + n), B("sc%d%s" % (t, c), n), 0.0, 11.0, A.is_gt, A.mult)
 
     def chain(t, c):
         lo, n = LO[c], NC[c]
         hi = lo + n
         y = "y" + c
-        first = t == 0 and c == "A"
+        first, final = (t, c) == (0, "A"), (t, c) == (ROUNDS - 1, "B")
         fl, dy, ee, ae, d0, d1, pl, sm = [R(k, lo, hi) for k in ("fl", "dy", "ee", "ae", "d0", "d1", "pl", "sm")]
         before = lo if c == "B" else C
         pp, xi = R("pp", 0, 1), R("xi", 0, 1)
         k0, k1 = lo // 16, hi // 16
         o1 = R("o1", k0, k1)
 
-        def distance():
-            scan(ee, fl, dy, 0.0 if first else R("ee", before - 1, before), A.add, A.subtract)
-            act(ae, ee, ACT.Abs, scale=TINY)
+        def on(i):
+            return "ch%d%s%d" % (t, c, i)
 
-        return [
-            lambda: scan(R(y, 1, n + 1), fl, R("zero", 0, n), BASE if first else xi, A.add, A.add),
-            lambda: scan(dy, R(y, 1, n + 1), R(y, 0, n), 0.0, A.max, A.subtract),
-            distance,
-            lambda: ts(xi, R("ee", hi - 1, hi), BASE, None, A.add),
-            lambda: ts(d0, ae, pp, None, A.subtract),
-            lambda: ts(d1, ae, pp, None, A.add),
-            lambda: scan(pl, d0, d1, 128.0 * TINY if first else R("pl", before - 1, before), A.max, A.min),
-            lambda: scan(sm, R("mask", 0, n), pl, 0.0, A.mult, A.add),
-            lambda: do("v", lambda e: e.tensor_tensor(o1[0], T.kt[:, 0:n // 16], T.sm[:, lo + 15:hi:16], A.subtract), [o1], [R("kt", 0, n // 16), sm]),
-            lambda: ts(R("off%d" % t, k0, k1), o1, R("sc", 0, 1), None, A.mult),
-        ]
+        scan(on(0), R(y, 1, n + 1), fl, R("zero", 0, n), BASE if first else xi, A.add, A.add)
+        scan(on(1), dy, R(y, 1, n + 1), R(y, 0, n), 0.0, A.max, A.subtract)
+        scan(on(2), ee, fl, dy, 0.0 if first else R("ee", before - 1, before), A.add, A.subtract)
+        act("ab%d%s" % (t, c), ae, ee, ACT.Abs, scale=TINY)
+        if not final:
+            act(on(3), xi, R("ee", hi - 1, hi), ACT.Identity, bias=BASE)
+        ts(on(4), d0, ae, pp, None, A.subtract)
+        if c == "B":
+            do(on(5), "s", lambda e: e.activation(d1[0], ae[0], ACT.Identity, bias=pp[0]), [d1], [ae, pp])
+        else:
+            ts(on(5), d1, ae, pp, None, A.add)
+        scan(on(6), pl, d0, d1, 128.0 * TINY if first else R("pl", before - 1, before), A.max, A.min)
+        scan(on(7), sm, R("mask", 0, n), pl, 0.0, A.mult, A.add)
+        do(on(8), "v", lambda e: e.tensor_tensor(o1[0], T.kt[:, 0:n // 16], T.sm[:, lo + 15:hi:16], A.subtract), [o1], [R("kt", 0, n // 16), sm])
+        ts(on(9), R("off%d" % t, k0, k1), o1, R("si", 15, 16), None, A.mult)
 
     def window(t, c, b):
         a, e = (0, C) if c == "A" else (CA, W)
@@ -271,137 +307,120 @@ def rank_program(g, core, T, topo):
         w, off = window(t, c, b)
         own = R("n%d%d" % (t % 2, b), LO[c], LO[c] + NC[c])
         z = zpiece(t, c, b)
-        do("v", lambda e: e.tensor_tensor(z[0], w[0].indirect(off[0]), own[0], A.add), [z], [w, off, own])
+        do("ga%d%s%d" % (t, c, b), "v", lambda e: e.tensor_tensor(z[0], w[0].indirect(off[0]), own[0], A.add), [z], [w, off, own])
 
     def gather(t, c, b):
         w, off = window(t, c, b)
         f = R("f%d%d" % (t % 2, b), LO[c], LO[c] + NC[c])
-        do("s", lambda e: e.activation(f[0], w[0].indirect(off[0]), ACT.Copy), [f], [w, off])
+        do("gs%d%s%d" % (t, c, b), "s", lambda e: e.activation(f[0], w[0].indirect(off[0]), ACT.Copy), [f], [w, off])
 
-    def add(t, c, b, bank):
-        tt(zpiece(t, c, b), R("bank%d" % bank, 0, NC[c]), R("f%d%d" % (t % 2, b), LO[c], LO[c] + NC[c]), A.add)
+    def add(t, c, b):
+        tt("ad%d%s%d" % (t, c, b), zpiece(t, c, b), B("un%d%s%d" % (t, c, b), NC[c]), R("f%d%d" % (t % 2, b), LO[c], LO[c] + NC[c]), A.add)
 
     def layer(t, c, b, bank):
-        mm(bank, NC[c], pair("cw", "sw", 128 * b, 128 * b + 128), pair("cz%d" % t, "sz%d" % t, LO[c], LO[c] + NC[c]))
+        mm("la%d%s%d" % (t, c, b), bank, NC[c], pair("cw", "sw", 128 * b, 128 * b + 128), pair("cz%d" % t, "sz%d" % t, LO[c], LO[c] + NC[c]))
 
-    def renew(t, c, b, bank):
+    def renew(t, c, b):
         lo, hi = 4 * LO[c], 4 * (LO[c] + NC[c])
-        tt(R("xt%d" % (t + 1), lo, hi, b), R("bank%d" % bank, 0, NC[c]), R("xt%d" % t, lo, hi, b), A.add)
+        tt("re%d%s%d" % (t, c, b), R("xt%d" % (t + 1), lo, hi, b), B("la%d%s%d" % (t, c, b), NC[c]), R("xt%d" % t, lo, hi, b), A.add)
+
+    def blend(t, c):
+        for b in range(4):
+            if b in GV[c]:
+                gather_add(t, c, b)
+            else:
+                gather(t, c, b)
+        for b in range(4):
+            if b not in GV[c]:
+                add(t, c, b)
 
     HA, HB, R0, R1, M, S = (0, 1), (2, 3), 4, 5, 6, 7
     DA = [M, M, HA[0], HA[1]]
     DB = [M, R1, HB[0], HB[1]]
 
-    quant_x(0, "A")
+    quant("qs", R("cq", 0, H), R("sq", 0, H), R("xt0", 0, 4 * H))
     send(0)
+    quant_x(0, "A")
     score(0, "A", R0)
-    constants1()
-    flags(0, "A", R0)
+    flags(0, "A")
+    quant_x(0, "B")
+    chain(0, "A")
     for b in (0, 2, 3):
         unpack(0, "A", b, DA[b])
-        cast(0, "A", b, DA[b])
-        if b == 0:
-            cast_own(0, "A", b, DA[b])
-    ca = chain(0, "A")
-    ca[0]()
-    constants2()
-    ca[1]()
-    quant_x(0, "B")
-    for i in (2, 3, 4, 5, 6):
-        ca[i]()
+        cast(0, "A", b)
+        cast_own(0, "A", b)
 
     for t in range(ROUNDS):
         last = t == ROUNDS - 1
         unpack(t, "A", 1, DA[1])
-        cast(t, "A", 1, DA[1])
-        cast_own(t, "A", 1, DA[1])
+        cast(t, "A", 1)
+        cast_own(t, "A", 1)
         for b in (1, 0):
             unpack(t, "B", b, DB[b])
-            cast(t, "B", b, DB[b])
+            cast(t, "B", b)
         score(t, "B", S)
         for b in (2, 3):
             unpack(t, "B", b, DB[b])
-            cast(t, "B", b, DB[b])
-        for i in (7, 8, 9):
-            ca[i]()
-        cb = chain(t, "B")
-        gather_add(t, "A", 1)
-        for b in (2, 3):
-            gather(t, "A", b)
-        for b in (1, 0):
-            cast_own(t, "B", b, DB[b])
-        flags(t, "B", S)
-        gather_add(t, "A", 0)
-        cb[0]()
-        for b in (2, 3):
-            add(t, "A", b, DA[b])
-            cb[b - 1]()
+            cast(t, "B", b)
+        blend(t, "A")
+        for b in (1, 0, 2, 3):
+            cast_own(t, "B", b)
+        flags(t, "B")
         quant_z(t, "A")
         ra = (R0, R1, HA[0], HA[1])
         for b in range(4):
             layer(t, "A", b, ra[b])
-        for i in (3, 4, 5):
-            cb[i]()
+        chain(t, "B")
         for b in range(4):
-            renew(t, "A", b, ra[b])
-            cb[6 + b]()
+            renew(t, "A", b)
         quant_x(t + 1, "A")
         tf = (M, S, HA[0], HA[1])
         for b in range(4):
             unpack_far(t, b, tf[b])
-            cast_far(t, b, tf[b])
+            cast_far(t, b)
         if not last:
             send(t + 1)
             score(t + 1, "A", R0)
-            ca = chain(t + 1, "A")
         else:
-            quant(R("cv", 0, 128), R("sv", 0, 128), R("vt", 0, 512))
-            mm(R0, CA, pair("cv", "sv", 0, 128), xcols(ROUNDS, "A"))
-        gather_add(t, "B", 0)
-        for b in (2, 3):
-            gather(t, "B", b)
-        if not last:
-            flags(t + 1, "A", R0)
-        gather_add(t, "B", 1)
-        if not last:
-            ca[0]()
-        for b in (2, 3):
-            add(t, "B", b, DB[b])
-            if not last:
-                ca[b - 1]()
+            quant("qv", R("cv", 0, 128), R("sv", 0, 128), R("vt", 0, 512))
+            mm("yA", R0, CA, pair("cv", "sv", 0, 128), xcols(ROUNDS, "A"))
+        blend(t, "B")
         quant_z(t, "B")
-        if not last:
-            for b in (0, 2, 3):
-                unpack(t + 1, "A", b, DA[b])
         rb = (R1, HB[0], HB[1], S)
         for b in range(4):
             layer(t, "B", b, rb[b])
         if not last:
-            for i in (3, 4, 5):
-                ca[i]()
+            flags(t + 1, "A")
             for b in (0, 2, 3):
-                cast(t + 1, "A", b, DA[b])
-                if b == 0:
-                    cast_own(t + 1, "A", b, DA[b])
+                unpack(t + 1, "A", b, DA[b])
+                cast(t + 1, "A", b)
+                cast_own(t + 1, "A", b)
+            chain(t + 1, "A")
         else:
-            act(R("yo", 0, CA), R("bank%d" % R0, 0, CA), ACT.Copy)
-            act(R("aof", 0, C), R("pl", 0, C), ACT.Identity, scale=-1.0 / TINY, bias=128.0)
+            act("eA", R("yo", 0, CA), B("yA", CA), ACT.Copy)
+            act("ea", R("aof", 0, C), R("pl", 0, C), ACT.Identity, scale=-1.0 / TINY, bias=128.0)
         for b in range(4):
-            renew(t, "B", b, rb[b])
-            if not last and b == 0:
-                ca[6]()
+            renew(t, "B", b)
         quant_x(t + 1, "B")
 
     xc, xs = "cx%d" % ROUNDS, "sx%d" % ROUNDS
-    mm(M, CB, pair("cv", "sv", 0, 128), xcols(ROUNDS, "B"))
-    dma("y", T.oc[:, 0:4 * CA], T[xc][:, 0:CA].bitcast(dt.uint8), [], [R(xc, 0, CA)])
-    dma("y", T.y[:, 0:CA], T.yo[:, 0:CA], [], [R("yo", 0, CA)])
-    dma("y", T.ao[:, :], T.aof[0:128:16, :], [], [R("aof", 0, C)])
-    vcopy(R("yo", CA, C), R("bank%d" % M, 0, CB))
-    dma("y", T.oc[:, 4 * CA:4 * C], T[xc][:, CA:C].bitcast(dt.uint8), [], [R(xc, CA, C)])
+    mm("yB", M, CB, pair("cv", "sv", 0, 128), xcols(ROUNDS, "B"))
+    dma("oA", "y", T.oc[:, 0:4 * CA], T[xc][:, 0:CA].bitcast(dt.uint8), [], [R(xc, 0, CA)])
+    dma("oy", "y", T.y[:, 0:CA], T.yo[:, 0:CA], [], [R("yo", 0, CA)])
+    dma("oa", "y", T.ao[:, :], T.aof[0:128:16, :], [], [R("aof", 0, C)])
+    do("eB", "v", lambda e: e.tensor_copy(T.yo[:, CA:C], B("yB", CB)[0]), [R("yo", CA, C)], [B("yB", CB)])
+    dma("oB", "y", T.oc[:, 4 * CA:4 * C], T[xc][:, CA:C].bitcast(dt.uint8), [], [R(xc, CA, C)])
     for k in range(4):
-        dma("sysy"[k], T.osc[4 * k:4 * k + 4, :], T[xs][32 * k:32 * k + 4, :], [], [R(xs, 0, C)])
-    dma("s", T.y[:, CA:C], T.yo[:, CA:C], [], [R("yo", CA, C)])
+        dma("os%d" % k, "sysy"[k], T.osc[4 * k:4 * k + 4, :], T[xs][32 * k:32 * k + 4, :], [], [R(xs, 0, C)])
+    dma("oz", "s", T.y[:, CA:C], T.yo[:, CA:C], [], [R("yo", CA, C)])
+
+    place = {n: i for i, n in enumerate(ORDER.split())}
+    if place:
+        calls.sort(key=lambda c: place[c[0]])
+    if not issue:
+        return calls
+    for c in calls:
+        start(c)
     for s in sorted(total):
         if s[:3] != "arr":
             g.wait_ge(T.sem[s], total[s])

from concourse.mybir import dt, AluOpType, ActivationFunctionType

ORDER = """
mi0 ldp zo ldu ldx0 ldx1 zz ldx2 ldv ldw mi1 eb0 yA0 eb1 ma0 hi0 ma1 yB0 zu ma2 hi1 pf pb0 eq0 qu pb1 rs eq1 kk0 ps eq3 pp u1 qs
u0 snd0 lds ma3 ma4 hi2 qx0A ic sc0A eq2 un0A0 fl0A un0A2 ca0A0 ch0A0 qx0B un0A3 ca0A2 ch0A1 sc0B ow0A0 ch0A2 kt un0B1 ab0A si
fl0B un0A1 ca0B1 ch0A5 un0B2 ch0A3 ch0A4 ca0A1 un0B3 ch0A6 ca0B2 ch0B0 ch0A7 ow0A1 ca0B3 ch0B1 ch0A8 un0B0 qv ca0A3 ch0A9 ch0B2
ca0B0 ga0A1 gs0A3 ga0A0 gs0A2 ad0A3 ch0B3 ow0B1 ad0A2 ab0B qz0A ch0B5 ow0B0 ch0B4 la0A3 ch0B6 ch0B7 la0A1 re0A3 la0A2 ch0B8 re0A1
la0A0 re0A2 re0A0 ch0B9 qx1A snd1 uf00 uf01 cf00 uf03 cf01 ga0B0 uf02 cf03 sc1A ga0B1 cf02 gs0B3 un1A3 fl1A gs0B2 un1A0 ad0B3 ch1A0
un1A2 ca1A0 ad0B2 ca1A3 qz0B ch1A1 ow1A0 la0B3 ch1A2 ca1A2 la0B1 re0B3 la0B2 ab1A re0B1 la0B0 re0B2 un1A1 re0B0 ch1A5 ca1A1 qx1B
ch1A4 ch1A3 sc1B ow1A1 ch1A6 un1B3 ch1A7 un1B1 fl1B ca1B3 un1B2 ch1A8 ca1B1 ch1B0 un1B0 ch1A9 ca1B2 ch1B1 ga1A1 gs1A3 ch1B2 ca1B0
ad1A3 gs1A2 ga1A0 ow1B0 ad1A2 ab1B uf10 ch1B5 uf11 qz1A ch1B3 ow1B1 ch1B4 la1A3 cf10 ch1B6 cf11 ch1B7 la1A2 re1A3 la1A1 ch1B8 re1A2
la1A0 re1A1 uf12 re1A0 uf13 cf12 ch1B9 qx2A cf13 gs1B2 ga1B1 un2A2 snd2 gs1B3 ga1B0 sc2A ca2A2 ad1B2 un2A3 ad1B3 un2A0 fl2A qz1B
ca2A0 ch2A0 la1B2 ow2A0 ch2A1 la1B0 re1B2 la1B3 ch2A2 re1B0 la1B1 ab2A re1B3 un2A1 ch2A3 re1B1 ch2A4 ca2A1 qx2B ch2A5 ow2A1 sc2B
ch2A6 un2B2 ca2A3 fl2B un2B0 ch2A7 ca2B2 ch2B0 un2B3 ch2A8 ca2B0 ch2B1 un2B1 ch2A9 ca2B3 ch2B2 ga2A0 ca2B1 gs2A2 ga2A1 gs2A3 ad2A2
ab2B ad2A3 ch2B5 ch2B4 qz2A ow2B0 ch2B6 ow2B1 uf21 ch2B7 ea la2A3 ch2B8 la2A2 cf21 re2A3 uf20 ch2B9 re2A2 uf23 cf20 ga2B1 la2A1 cf23
ga2B0 uf22 gs2B3 la2A0 re2A1 cf22 re2A0 gs2B2 ad2B3 qx3A ad2B2 yA oA oa qz2B eA la2B0 la2B3 oy re2B0 la2B1 re2B3 la2B2 re2B1 re2B2
qx3B yB oB os0 os3 os2 os1 eB oz
"""
GV = {"A": (0, 1), "B": (0, 1)}
BANKS = {}

N = 8
CA, CB, C, H, W = 192, 128, 320, 128, 448
LO = {"A": 0, "B": CA}
NC = {"A": CA, "B": CB}
ROUNDS = 3
ENGINES = slice(0, 8)
TINY = 2.0 ** -30
BASE = 49152.0

F32, B16, I32, U16, U8, X4 = "float32", "bfloat16", "int32", "uint16", "uint8", "float8_e4m3fn_x4"
SCRATCH = {
    "ut": ("sbuf", [128, 512], B16), "vt": ("sbuf", [128, 512], B16),
    "cu": ("sbuf", [128, 128], X4), "su": ("sbuf", [128, 128], U8),
    "cu0": ("sbuf", [128, 128], X4), "su0": ("sbuf", [128, 128], U8),
    "cv": ("sbuf", [128, 128], X4), "sv": ("sbuf", [128, 128], U8),
    "cw": ("sbuf", [128, 512], X4), "sw": ("sbuf", [128, 512], U8),
    "cq": ("sbuf", [128, H], X4), "sq": ("sbuf", [128, H], U8),
    "eb": ("sbuf", [128, 516], B16), "ce": ("sbuf", [128, 512], X4), "se": ("sbuf", [128, 512], U8),
    "offz": ("sbuf", [128, 8], U16), "zero": ("sbuf", [128, CA], B16),
    "mi": ("sbuf", [128, 16], I32), "mask": ("sbuf", [128, CA], B16), "hit": ("sbuf", [128, 16], B16),
    "mask2": ("sbuf", [128, 16], B16), "hit2": ("sbuf", [128, 16], B16),
    "rs": ("sbuf", [128, 16], F32), "si": ("sbuf", [128, 16], F32), "ic": ("sbuf", [128, 1], F32),
    "kk": ("sbuf", [128, 12], F32), "kt": ("sbuf", [128, 12], F32),
    "prow": ("sbuf", [1, 8], I32), "pf": ("sbuf", [1, 8], F32), "pb": ("sbuf", [128, 8], F32), "pj": ("sbuf", [128, 8], F32),
    "ps": ("sbuf", [128, 1], F32), "pp": ("sbuf", [128, 1], B16), "xi": ("sbuf", [128, 1], F32),
    "fl": ("sbuf", [128, C], B16), "yA": ("sbuf", [128, CA + 8], B16), "yB": ("sbuf", [128, CB + 8], B16),
    "dy": ("sbuf", [128, C], B16), "ee": ("sbuf", [128, C], B16), "ae": ("sbuf", [128, C], B16),
    "d0": ("sbuf", [128, C], B16), "d1": ("sbuf", [128, C], B16), "pl": ("sbuf", [128, C], B16),
    "sm": ("sbuf", [128, C], B16), "o1": ("sbuf", [128, 20], F32),
    "aof": ("sbuf", [128, C], F32), "yo": ("sbuf", [128, C], F32),
}
for _t in range(ROUNDS + 1):
    SCRATCH["xt%d" % _t] = ("sbuf", [128, 4 * C], B16)
    SCRATCH["cx%d" % _t] = ("sbuf", [128, C], X4)
    SCRATCH["sx%d" % _t] = ("sbuf", [128, C], U8)
for _t in range(ROUNDS):
    SCRATCH["lc%d" % _t] = ("sbuf", [128, H], X4)
    SCRATCH["ls%d" % _t] = ("sbuf", [128, H], U8)
    SCRATCH["zt%d" % _t] = ("sbuf", [128, 4 * C], B16)
    SCRATCH["cz%d" % _t] = ("sbuf", [128, C], X4)
    SCRATCH["sz%d" % _t] = ("sbuf", [128, C], U8)
    SCRATCH["off%d" % _t] = ("sbuf", [128, 20], U16)
for _t in range(2):
    for _b in range(4):
        SCRATCH["w%d%d" % (_t, _b)] = ("sbuf", [128, W], B16)
        SCRATCH["f%d%d" % (_t, _b)] = ("sbuf", [128, C], B16)
        SCRATCH["n%d%d" % (_t, _b)] = ("sbuf", [128, C], B16)
for _b in range(8):
    SCRATCH["bank%d" % _b] = ("psum", [128, 512], F32)
NDMA = 17
SEMAPHORES = ["c_pe", "c_v", "c_s", "c_g"] + ["dma%d" % _i for _i in range(NDMA)] + ["arr%d" % _t for _t in range(ROUNDS)] + ["left%d" % _t for _t in range(ROUNDS)]


def rank_program(g, core, T, topo):
    if T.rank_of(core) is not None:
        build(g, core, T, topo, True)


def build(g, core, T, topo, issue):
    rank = T.rank_of(core)
    A, ACT = AluOpType, ActivationFunctionType
    queue = {"pe": g.tensor, "v": g.vector, "s": g.scalar, "y": g.sync, "g": g}
    dst, src = T.cores[(rank - 1) % N], T.cores[(rank + 1) % N]
    rid, pidn = topo.addr(dst)[0], topo.addr(dst)[1]
    mine, theirs = topo.engines(core, dst)[ENGINES], topo.engines(src, core)[ENGINES]
    mask_out = sum(1 << e for e in mine)

    known = {q: {} for q in queue}
    count, total = {q: 0 for q in queue}, {}
    history = {}
    ndma, serial = [0], [0]
    calls, taken = [], {}

    def R(name, lo, hi, phase=None):
        ap = T[name][:, lo:hi] if phase is None else T[name][:, lo + phase:hi:4]
        return (ap, name, lo, hi, phase)

    def order(q, reads, writes):
        need = {}
        for refs, w in ((reads, False), (writes, True)):
            for (ap, name, lo, hi, ph) in refs:
                for (l2, h2, p2, w2, call) in history.get(name, []):
                    if (w or w2 or name[:4] == "bank") and lo < h2 and l2 < hi and (ph is None or p2 is None or ph == p2):
                        need[call[0]] = call
        for i in sorted(need, reverse=True):
            call = need[i]
            if known[q].get(call[1], 0) < call[2]:
                queue[q].wait_ge(T.sem[call[1]], call[2])
                for s, v in call[3].items():
                    known[q][s] = max(known[q].get(s, 0), v)

    def record(q, sem, val, reads, writes):
        clock = dict(known[q]) if q else {}
        clock[sem] = max(val, clock.get(sem, 0))
        total[sem] = max(val, total.get(sem, 0))
        serial[0] += 1
        call = (serial[0], sem, val, clock)
        for refs, w in ((reads, False), (writes, True)):
            for (ap, name, lo, hi, ph) in refs:
                history.setdefault(name, []).append((lo, hi, ph, w, call))

    def put(name, q, kind, fn, writes, reads):
        calls.append((name, q, kind, fn, writes, reads))

    def do(name, q, fn, writes, reads):
        put(name, q, "c", fn, writes, reads)

    def dma(name, q, out, in_, writes=(), reads=()):
        put(name, q, "d", lambda e: e.dma_start(out, in_), writes, reads)

    def start(call):
        name, q, kind, fn, writes, reads = call
        order(q, reads, writes)
        if kind == "c":
            count[q] += 1
            fn(queue[q]).then_inc(T.sem["c_" + q], 1)
            record(q, "c_" + q, count[q], reads, writes)
        elif kind == "d":
            sem = "dma%d" % ndma[0]
            ndma[0] += 1
            fn(queue[q]).then_inc(T.sem[sem], 16)
            record(q, sem, 16, reads, writes)
        else:
            fn(queue[q])
            total["left" + kind] = 2 * len(mine)
            record(None, "arr" + kind, 2 * len(theirs), [], writes)

    def B(use, n):
        return R("bank%d" % BANKS.get(use, taken.get(use)), 0, n)

    def mm(name, bank, n, st, mv):
        taken[name] = bank
        out = B(name, n)
        do(name, "pe", lambda e: e.matmul_mx(out[0], st[0][0], st[1][0], mv[0][0], mv[1][0], True, True), [out], [st[0], st[1], mv[0], mv[1]])

    def quant(name, c, s, t):
        do(name, "v", lambda e: e.quantize_mx(c[0], s[0], t[0]), [c, s], [t])

    def ts(name, out, in0, s1, s2, op0, op1=None):
        a1 = s1[0] if isinstance(s1, tuple) else s1
        a2 = s2[0] if isinstance(s2, tuple) else s2
        reads = [in0] + [s for s in (s1, s2) if isinstance(s, tuple)]
        if op1 is None:
            do(name, "v", lambda e: e.tensor_scalar(out[0], in0[0], a1, None, op0), [out], reads)
        else:
            do(name, "v", lambda e: e.tensor_scalar(out[0], in0[0], a1, a2, op0, op1), [out], reads)

    def tt(name, out, a, b, op):
        do(name, "v", lambda e: e.tensor_tensor(out[0], a[0], b[0], op), [out], [a, b])

    def scan(name, out, a, b, init, op0, op1):
        i = init[0] if isinstance(init, tuple) else init
        do(name, "v", lambda e: e.tensor_tensor_scan(out[0], a[0], b[0], i, op0, op1), [out], [a, b] + ([init] if isinstance(init, tuple) else []))

    def fill(name, out, val):
        do(name, "v", lambda e: e.memset(out[0], val), [out], [])

    def act(name, out, in_, func, **kw):
        do(name, "s", lambda e: e.activation(out[0], in_[0], func, **kw), [out], [in_])

    def pair(c, s, lo, hi):
        return R(c, lo, hi), R(s, lo, hi)

    dma("ldx0", "y", T.xt0[:, 0:4 * H], T.x[:, 0:4 * H], [R("xt0", 0, 4 * H)])
    dma("ldu", "s", T.ut[:, 0:32], T.u[:, 0:32], [R("ut", 0, 32)])
    dma("ldp", "y", T.prow[0:1, :], T.p[:], [R("prow", 0, 8)])
    dma("ldx1", "s", T.xt0[:, 4 * H:4 * CA], T.x[:, 4 * H:4 * CA], [R("xt0", 4 * H, 4 * CA)])
    dma("ldx2", "y", T.xt0[:, 4 * CA:4 * C], T.x[:, 4 * CA:4 * C], [R("xt0", 4 * CA, 4 * C)])
    dma("ldw", "y", T.cw[:, 0:512].bitcast(dt.uint8), T.wc[:, :], [R("cw", 0, 512)])
    dma("lds", "s", T.sw[:, :], T.ws[:, :], [R("sw", 0, 512)])
    dma("ldv", "y", T.vt[:, :], T.v[:, :], [R("vt", 0, 512)])

    eb, mi, pb = R("eb", 0, 516), R("mi", 0, 16), R("pb", 0, 8)
    fill("eb0", eb, 0.0)
    do("mi0", "g", lambda e: e.iota(T.mi[:, :], [[-1, 16]], 16, 1), [mi], [])
    do("eb1", "g", lambda e: e.affine_select(T.eb[:, :], T.eb[:, :], [[-1, 516]], A.not_equal, 2.0 ** -6, 3, 4), [eb], [eb])
    do("kk0", "g", lambda e: e.iota(T.kk[:, :], [[16, 12]], 128, 0, allow_small_or_imprecise_dtypes=True), [R("kk", 0, 12)], [])
    fill("zo", R("offz", 0, 8), 0)
    fill("zu", R("ut", 32, 512), 0.0)
    fill("zz", R("zero", 0, CA), 0.0)
    fill("yA0", R("yA", 0, 1), BASE)
    fill("yB0", R("yB", 0, 1), BASE)
    for b in range(4):
        quant("eq%d" % b, R("ce", 128 * b, 128 * b + 128), R("se", 128 * b, 128 * b + 128), R("eb", 3 - b, 515 - b))
    quant("qu", R("cu", 0, 128), R("su", 0, 128), R("ut", 0, 512))
    do("u0", "v", lambda e: e.tensor_copy(T.cu0[:, 0:128].bitcast(dt.uint32), T.cu[:, 0:8].bitcast(dt.uint32).indirect(T.offz[:, 0:8])), [R("cu0", 0, 128)], [R("cu", 0, 8), R("offz", 0, 8)])
    do("u1", "s", lambda e: e.activation(T.su0[:, 0:128], T.su[:, 0:8].indirect(T.offz[:, 0:8]), ACT.Copy), [R("su0", 0, 128)], [R("su", 0, 8), R("offz", 0, 8)])
    ts("mi1", mi, mi, 15, None, A.bitwise_and)
    ts("ma0", R("mask", 0, 16), mi, 0.0, 512.0, A.is_gt, A.mult)
    for k, (lo, hi, n) in enumerate(((16, 32, 16), (32, 64, 32), (64, 128, 64), (128, CA, CA - 128))):
        act("ma%d" % (k + 1), R("mask", lo, hi), R("mask", 0, n), ACT.Copy)
    ts("hi0", R("hit", 0, 16), mi, 0.0, TINY, A.is_equal, A.mult)
    act("hi1", R("hit2", 0, 16), R("hit", 0, 16), ACT.Copy, scale=2.0 ** 60)
    act("hi2", R("mask2", 0, 16), R("mask", 0, 16), ACT.Copy, scale=2.0 ** -18)
    scan("rs", R("rs", 0, 16), R("mask", 0, 16), R("hit", 0, 16), 0.0, A.mult, A.add)
    scan("si", R("si", 0, 16), R("mask2", 0, 16), R("hit2", 0, 16), 0.0, A.mult, A.add)
    ts("ic", R("ic", 0, 1), R("mi", 0, 1), 0.375, None, A.add)
    ts("kt", R("kt", 0, 12), R("kk", 0, 12), R("ic", 0, 1), R("rs", 15, 16), A.add, A.mult)
    do("pf", "v", lambda e: e.tensor_scalar(T.pf[0:1, :], T.prow[0:1, :], TINY, None, A.mult), [R("pf", 0, 8)], [R("prow", 0, 8)])
    do("pb0", "g", lambda e: e.partition_broadcast(T.pb[:, :], T.pf[0:1, :], 128), [pb], [R("pf", 0, 8)])
    do("pb1", "g", lambda e: e.affine_select(T.pb[:, :], T.pb[:, :], [[-16, 8]], A.is_ge, 0.0, 0, 1), [pb], [pb])
    do("ps", "s", lambda e: e.activation(T.pj[:, :], T.pb[:, :], ACT.Copy, accum_out=T.ps[:, :]), [R("pj", 0, 8), R("ps", 0, 1)], [pb])
    act("pp", R("pp", 0, 1), R("ps", 0, 1), ACT.Copy)

    def send(t):
        c, s = pair("cx%d" % t, "sx%d" % t, 0, H) if t else pair("cq", "sq", 0, H)
        rs, ls = T.sem["arr%d" % t], T.sem["left%d" % t]

        def write(e):
            e.remote_dma(out_ap=T["lc%d" % t][:, 0:H].bitcast(dt.uint8), in_ap=c[0].bitcast(dt.uint8), remote_sem=rs, local_sem=ls, pid=pidn, routing_id=rid, dma_engine_mask=mask_out)
            e.remote_dma(out_ap=T["ls%d" % t][:, 0:H], in_ap=s[0], remote_sem=rs, local_sem=ls, pid=pidn, routing_id=rid, dma_engine_mask=mask_out)
        put("snd%d" % t, "g", "%d" % t, write, [R("lc%d" % t, 0, H), R("ls%d" % t, 0, H)], [c, s])

    def quant_x(t, c):
        lo, hi = LO[c], LO[c] + NC[c]
        quant("qx%d%s" % (t, c), R("cx%d" % t, lo, hi), R("sx%d" % t, lo, hi), R("xt%d" % t, 4 * lo, 4 * hi))

    def quant_z(t, c):
        lo, hi = LO[c], LO[c] + NC[c]
        quant("qz%d%s" % (t, c), R("cz%d" % t, lo, hi), R("sz%d" % t, lo, hi), R("zt%d" % t, 4 * lo, 4 * hi))

    def xcols(t, c):
        return pair("cx%d" % t, "sx%d" % t, LO[c], LO[c] + NC[c])

    def score(t, c, bank):
        mm("sc%d%s" % (t, c), bank, NC[c], pair("cu0", "su0", 0, 128), xcols(t, c))

    def unpack(t, c, b, bank):
        mm("un%d%s%d" % (t, c, b), bank, NC[c], pair("ce", "se", 128 * b, 128 * b + 128), xcols(t, c))

    def cast(t, c, b):
        act("ca%d%s%d" % (t, c, b), R("w%d%d" % (t % 2, b), LO[c], LO[c] + NC[c]), B("un%d%s%d" % (t, c, b), NC[c]), ACT.Copy)

    def cast_own(t, c, b):
        if b in GV[c]:
            act("ow%d%s%d" % (t, c, b), R("n%d%d" % (t % 2, b), LO[c], LO[c] + NC[c]), B("un%d%s%d" % (t, c, b), NC[c]), ACT.Copy)

    def unpack_far(t, b, bank):
        mm("uf%d%d" % (t, b), bank, H, pair("ce", "se", 128 * b, 128 * b + 128), pair("lc%d" % t, "ls%d" % t, 0, H))

    def cast_far(t, b):
        act("cf%d%d" % (t, b), R("w%d%d" % (t % 2, b), C, W), B("uf%d%d" % (t, b), H), ACT.Copy)

    def flags(t, c):
        lo, n = LO[c], NC[c]
        ts("fl%d%s" % (t, c), R("fl", lo, lo + n), B("sc%d%s" % (t, c), n), 0.0, 11.0, A.is_gt, A.mult)

    def chain(t, c):
        lo, n = LO[c], NC[c]
        hi = lo + n
        y = "y" + c
        first, final = (t, c) == (0, "A"), (t, c) == (ROUNDS - 1, "B")
        fl, dy, ee, ae, d0, d1, pl, sm = [R(k, lo, hi) for k in ("fl", "dy", "ee", "ae", "d0", "d1", "pl", "sm")]
        before = lo if c == "B" else C
        pp, xi = R("pp", 0, 1), R("xi", 0, 1)
        k0, k1 = lo // 16, hi // 16
        o1 = R("o1", k0, k1)

        def on(i):
            return "ch%d%s%d" % (t, c, i)

        scan(on(0), R(y, 1, n + 1), fl, R("zero", 0, n), BASE if first else xi, A.add, A.add)
        scan(on(1), dy, R(y, 1, n + 1), R(y, 0, n), 0.0, A.max, A.subtract)
        scan(on(2), ee, fl, dy, 0.0 if first else R("ee", before - 1, before), A.add, A.subtract)
        act("ab%d%s" % (t, c), ae, ee, ACT.Abs, scale=TINY)
        if not final:
            act(on(3), xi, R("ee", hi - 1, hi), ACT.Identity, bias=BASE)
        ts(on(4), d0, ae, pp, None, A.subtract)
        if c == "B":
            do(on(5), "s", lambda e: e.activation(d1[0], ae[0], ACT.Identity, bias=pp[0]), [d1], [ae, pp])
        else:
            ts(on(5), d1, ae, pp, None, A.add)
        scan(on(6), pl, d0, d1, 128.0 * TINY if first else R("pl", before - 1, before), A.max, A.min)
        scan(on(7), sm, R("mask", 0, n), pl, 0.0, A.mult, A.add)
        do(on(8), "v", lambda e: e.tensor_tensor(o1[0], T.kt[:, 0:n // 16], T.sm[:, lo + 15:hi:16], A.subtract), [o1], [R("kt", 0, n // 16), sm])
        ts(on(9), R("off%d" % t, k0, k1), o1, R("si", 15, 16), None, A.mult)

    def window(t, c, b):
        a, e = (0, C) if c == "A" else (CA, W)
        return R("w%d%d" % (t % 2, b), a, e), R("off%d" % t, LO[c] // 16, (LO[c] + NC[c]) // 16)

    def zpiece(t, c, b):
        return R("zt%d" % t, 4 * LO[c], 4 * (LO[c] + NC[c]), b)

    def gather_add(t, c, b):
        w, off = window(t, c, b)
        own = R("n%d%d" % (t % 2, b), LO[c], LO[c] + NC[c])
        z = zpiece(t, c, b)
        do("ga%d%s%d" % (t, c, b), "v", lambda e: e.tensor_tensor(z[0], w[0].indirect(off[0]), own[0], A.add), [z], [w, off, own])

    def gather(t, c, b):
        w, off = window(t, c, b)
        f = R("f%d%d" % (t % 2, b), LO[c], LO[c] + NC[c])
        do("gs%d%s%d" % (t, c, b), "s", lambda e: e.activation(f[0], w[0].indirect(off[0]), ACT.Copy), [f], [w, off])

    def add(t, c, b):
        tt("ad%d%s%d" % (t, c, b), zpiece(t, c, b), B("un%d%s%d" % (t, c, b), NC[c]), R("f%d%d" % (t % 2, b), LO[c], LO[c] + NC[c]), A.add)

    def layer(t, c, b, bank):
        mm("la%d%s%d" % (t, c, b), bank, NC[c], pair("cw", "sw", 128 * b, 128 * b + 128), pair("cz%d" % t, "sz%d" % t, LO[c], LO[c] + NC[c]))

    def renew(t, c, b):
        lo, hi = 4 * LO[c], 4 * (LO[c] + NC[c])
        tt("re%d%s%d" % (t, c, b), R("xt%d" % (t + 1), lo, hi, b), B("la%d%s%d" % (t, c, b), NC[c]), R("xt%d" % t, lo, hi, b), A.add)

    def blend(t, c):
        for b in range(4):
            if b in GV[c]:
                gather_add(t, c, b)
            else:
                gather(t, c, b)
        for b in range(4):
            if b not in GV[c]:
                add(t, c, b)

    HA, HB, R0, R1, M, S = (0, 1), (2, 3), 4, 5, 6, 7
    DA = [M, M, HA[0], HA[1]]
    DB = [M, R1, HB[0], HB[1]]

    quant("qs", R("cq", 0, H), R("sq", 0, H), R("xt0", 0, 4 * H))
    send(0)
    quant_x(0, "A")
    score(0, "A", R0)
    flags(0, "A")
    quant_x(0, "B")
    chain(0, "A")
    for b in (0, 2, 3):
        unpack(0, "A", b, DA[b])
        cast(0, "A", b)
        cast_own(0, "A", b)

    for t in range(ROUNDS):
        last = t == ROUNDS - 1
        unpack(t, "A", 1, DA[1])
        cast(t, "A", 1)
        cast_own(t, "A", 1)
        for b in (1, 0):
            unpack(t, "B", b, DB[b])
            cast(t, "B", b)
        score(t, "B", S)
        for b in (2, 3):
            unpack(t, "B", b, DB[b])
            cast(t, "B", b)
        blend(t, "A")
        for b in (1, 0, 2, 3):
            cast_own(t, "B", b)
        flags(t, "B")
        quant_z(t, "A")
        ra = (R0, R1, HA[0], HA[1])
        for b in range(4):
            layer(t, "A", b, ra[b])
        chain(t, "B")
        for b in range(4):
            renew(t, "A", b)
        quant_x(t + 1, "A")
        tf = (M, S, HA[0], HA[1])
        for b in range(4):
            unpack_far(t, b, tf[b])
            cast_far(t, b)
        if not last:
            send(t + 1)
            score(t + 1, "A", R0)
        else:
            quant("qv", R("cv", 0, 128), R("sv", 0, 128), R("vt", 0, 512))
            mm("yA", R0, CA, pair("cv", "sv", 0, 128), xcols(ROUNDS, "A"))
        blend(t, "B")
        quant_z(t, "B")
        rb = (R1, HB[0], HB[1], S)
        for b in range(4):
            layer(t, "B", b, rb[b])
        if not last:
            flags(t + 1, "A")
            for b in (0, 2, 3):
                unpack(t + 1, "A", b, DA[b])
                cast(t + 1, "A", b)
                cast_own(t + 1, "A", b)
            chain(t + 1, "A")
        else:
            act("eA", R("yo", 0, CA), B("yA", CA), ACT.Copy)
            act("ea", R("aof", 0, C), R("pl", 0, C), ACT.Identity, scale=-1.0 / TINY, bias=128.0)
        for b in range(4):
            renew(t, "B", b)
        quant_x(t + 1, "B")

    xc, xs = "cx%d" % ROUNDS, "sx%d" % ROUNDS
    mm("yB", M, CB, pair("cv", "sv", 0, 128), xcols(ROUNDS, "B"))
    dma("oA", "y", T.oc[:, 0:4 * CA], T[xc][:, 0:CA].bitcast(dt.uint8), [], [R(xc, 0, CA)])
    dma("oy", "y", T.y[:, 0:CA], T.yo[:, 0:CA], [], [R("yo", 0, CA)])
    dma("oa", "y", T.ao[:, :], T.aof[0:128:16, :], [], [R("aof", 0, C)])
    do("eB", "v", lambda e: e.tensor_copy(T.yo[:, CA:C], B("yB", CB)[0]), [R("yo", CA, C)], [B("yB", CB)])
    dma("oB", "y", T.oc[:, 4 * CA:4 * C], T[xc][:, CA:C].bitcast(dt.uint8), [], [R(xc, CA, C)])
    for k in range(4):
        dma("os%d" % k, "sysy"[k], T.osc[4 * k:4 * k + 4, :], T[xs][32 * k:32 * k + 4, :], [], [R(xs, 0, C)])
    dma("oz", "s", T.y[:, CA:C], T.yo[:, CA:C], [], [R("yo", CA, C)])

    place = {n: i for i, n in enumerate(ORDER.split())}
    if place:
        calls.sort(key=lambda c: place[c[0]])
    if not issue:
        return calls
    for c in calls:
        start(c)
    for s in sorted(total):
        if s[:3] != "arr":
            g.wait_ge(T.sem[s], total[s])
